import numpy as np, ml_dtypes
CORES = [5,29,101,125,133,157,229,253]
N = 8
import mx_ref
BF = ml_dtypes.bfloat16
def gentries(a):
    return np.ascontiguousarray(a.reshape(8, 16, -1).transpose(0, 2, 1)).reshape(8, -1)
def gtable(e):
    e = np.asarray(e); return np.ascontiguousarray(e.reshape(8, -1, 16).transpose(0, 2, 1)).reshape(128, -1).astype(np.int32)
def gcols(t, e):
    v = np.concatenate([t.reshape(8, 16, -1, 4), np.zeros((8, 16, 1, 4), BF)], axis=2)
    return np.ascontiguousarray(np.stack([v[g][:, e[g]] for g in range(8)])).reshape(128, -1)
def tile(rs):
    return np.stack(rs, axis=2).reshape(128, -1).astype(BF)
def pick(q, e):
    c = np.concatenate([q[0].reshape(128, -1, 4), np.zeros((128, 1, 4), np.uint8)], axis=1); s = np.concatenate([q[1], np.ones((16, 1), np.uint8)], axis=1)
    return (np.ascontiguousarray(c[:, e].reshape(128, -1)), np.ascontiguousarray(s[:, e]))
def join(*qs):
    return (np.concatenate([q[0] for q in qs], axis=1), np.concatenate([q[1] for q in qs], axis=1))
def put(q, e, v):
    c, s = q[0].reshape(128, -1, 4).copy(), q[1].copy(); c[:, e] = v[0].reshape(128, -1, 4); s[:, e] = v[1]
    return (c.reshape(128, -1), s)
def pk(c, s):
    return (np.ascontiguousarray(c), mx_ref.live(s))
def emit(q):
    return q[0], q[1]
def packed(v, rng):
    q = [mx_ref.quantize(np.ascontiguousarray(v[r])) for r in range(N)]
    return np.stack([a for a, b in q]), np.stack([mx_ref.plane(b, rng) for a, b in q])
def values_of_codes():
    e, c = np.zeros((128, 128, 4), np.float32), np.zeros((128, 2, 4), np.uint8)
    e[np.arange(128), np.arange(128), 0] = 1
    c[:127, :, 0] = np.arange(256).reshape(2, 128).T[:127]
    return mx_ref.matmul(mx_ref.quantize(e.reshape(128, 512).astype(BF)), (c.reshape(128, 8), np.full((16, 2), 127, np.uint8))).T.reshape(-1).astype(np.float64)
CODE_VALUE, SCALE_VALUE = values_of_codes(), 2.0 ** (np.arange(256) - 127.0)
def decode(q):
    return (CODE_VALUE[q[0]].reshape(16, 8, -1, 4) * SCALE_VALUE[q[1]][:, None, :, None] + 0.0).reshape(128, -1).astype(np.float32)
def f(rng, *shape):
    return mx_ref.flush((rng.standard_normal(shape, dtype=np.float32) * np.exp2(rng.integers(-2, 3, shape[:-1] + (1,)))).astype(BF))
def wide(rng, *shape, cols=0):
    v = rng.standard_normal(shape, dtype=np.float32) * np.exp2(rng.integers(-12, 13, shape)).astype(np.float32)
    if cols: v *= np.repeat(np.exp2(rng.integers(-cols, cols + 1, shape[:-2] + (1, shape[-1] // 4))) * (rng.random(shape[:-2] + (1, shape[-1] // 4)) > 0.0625), 4, axis=-1).astype(np.float32)
    return mx_ref.flush(v.astype(BF))
C, HALF = 320, 160
STEP = [4, 1, 2]
def big(v):
    v = v.astype(np.float32)
    v[np.abs(v) < np.float32(2.0 ** -16)] = 0
    return v.astype(BF)
def numbers_of(rng):
    return {"x": big(f(rng, N, 128, 4 * C)), "u": np.array(f(rng, N, 128, 512)), "v": np.array(f(rng, N, 128, 512))}
def lists(rng):
    e = np.tile(np.arange(C), (N, 8, 1))
    o = rng.permuted(e, axis=2)
    m = np.zeros((N, 8, C), np.int64)
    np.put_along_axis(m, o, o[:, :, np.arange(C) ^ 1], axis=2)
    return rng.permuted(e, axis=2), m
def stored(q, m):
    return {"gq": np.stack([gtable(q[r]) for r in range(N)]), "gm": np.stack([gtable(m[r]) for r in range(N)])}
def layers(rng):
    return big(f(rng, N, 128, 2048)).reshape(N, 8, 16, 4, 8, 16, 4)
def no_layers():
    return np.zeros((N, 8, 16, 4, 8, 16, 4), np.float32)
def weights(rng, w):
    c, p = packed(np.ascontiguousarray(w.astype(BF)).reshape(N, 128, 2048), rng)
    return {"wc": c, "ws": p}
def setup_inputs(rng):
    return {**numbers_of(rng), **stored(*lists(rng)), **weights(rng, layers(rng))}
def setup_inputs_ties(rng):
    d = numbers_of(rng)
    o = rng.permutation(N)
    q, m = lists(rng)
    k = rng.integers(-1, 2, (N, 8, C)).astype(np.float32)
    k[o[0], rng.permutation(8)[:4]] = 0
    k[o[1]] = np.where(rng.permutation(8) < 4, 1, -1)[:, None]
    k[o[3]] = np.where(np.arange(C) < HALF, 1, -3)
    for g in range(8):
        a, b, p = rng.permutation(HALF), HALF + rng.permutation(HALF), rng.permutation(HALF)
        q[o[3], g] = np.concatenate([a, b] if g == 0 else [b, a])
        m[o[3], g, :HALF] = HALF + p
        m[o[3], g, HALF + p] = np.arange(HALF)
    x = d["x"].reshape(N, 8, 16, C, 4)
    x[:, :, 0] = 0
    x[:, :, 0, :, 0] = k.astype(BF)
    u = d["u"].reshape(N, 128, 128, 4)
    u[:, :, ::16] = 0
    for h in range(0, 128, 16): u[:, h, h, 0] = 1
    w = layers(rng)
    w[:, :, :, :, :, 0] = 0
    return {"x": x.reshape(N, 128, 4 * C), "u": u.reshape(N, 128, 512), "v": d["v"], **stored(q, m), **weights(rng, w)}
def setup_inputs_near(rng):
    d = numbers_of(rng)
    o = rng.permutation(N) % 2
    k = np.where(o == 0, 2.0 ** -30, 1.0)
    x = np.zeros((N, 8, 16, C, 4))
    s = rng.integers(-1, 2, (N, 8, C)) * k[:, None, None]
    x[:, :, 0, :, 0] = 1.125 * s
    x[:, :, 1, :, 0] = -1.25 * s
    x[:, :, 7, :, 0] = 2.0 ** -30
    x[:, :, 8, :, 0] = 2.0 ** -30
    for r in range(N):
        at = [0, C - 1, int(rng.integers(C)), int(rng.integers(C))]
        for g, j in zip(rng.permutation(8)[:4], at): x[r, g, 0, j, 0] = 2.0 ** 30 * rng.choice([-1.0, 1.0])
    u = d["u"].reshape(N, 128, 128, 4)
    u[:, :, ::16] = 0
    for h in range(0, 128, 16):
        u[:, h, h, 0] = (1.125 * k).astype(np.float32).astype(BF)
        u[:, h + 1, h, 0] = k.astype(np.float32).astype(BF)
        u[:, h + 9, h, 0] = 2.0 ** -30
    w = no_layers()
    for g in range(8):
        w[:, g, 8, 0, g, 8, 0] = 32
        w[:, g, 1, 0, g, 9, 0] = np.where(o == 0, 2.0 ** -9, 2.0 ** -30)
    return {"x": x.astype(np.float32).reshape(N, 128, 4 * C).astype(BF), "u": u.reshape(N, 128, 512), "v": d["v"], **stored(*lists(rng)), **weights(rng, w)}
def setup_inputs_odd(rng):
    d = numbers_of(rng)
    x = (1.0 + (2 * rng.integers(0, 64, (N, 8, 16, C, 4)) + 1) * 2.0 ** -7) * np.exp2(-rng.integers(0, 7, (N, 8, 16, C, 4)).astype(np.float64)) * rng.choice([-1.0, 1.0], (N, 8, 16, C, 4))
    e = rng.choice([-1.0, 1.0], (N, 8, C)) * 2.0 ** -8
    n = rng.integers(0, 2, (N, 8, C))
    x[:, :, 8:] = 0
    x[:, :, 0, :, 0] = 1.96875 * 2.0 ** 8 * rng.choice([-1.0, 1.0], (N, 8, 1))
    x[:, :, 1, :, 0] = np.where(n == 0, 5.0, 7.0) * e
    x[:, :, 8, :, 0] = np.where(n == 0, -4.5, -7.5) * e
    x[:, :, 10, :, 0] = 1.125 * 2.0 ** -2
    u = d["u"].reshape(N, 128, 128, 4)
    u[:, :, ::16] = 0
    for h in range(0, 128, 16):
        u[:, h + 1, h, 0] = 1
        u[:, h + 8, h, 0] = 1
    w = no_layers()
    for g in range(8):
        w[:, g, 10, 0, g, 9, 0] = 1.75 * 2.0 ** 5
        for b in range(4): w[:, g, 10, b, g, 11:, 0] = rng.choice([1.125, 1.5, 2.0], (N, 5)) * 2.0 ** -9
    return {"x": x.astype(np.float32).reshape(N, 128, 4 * C).astype(BF), "u": u.reshape(N, 128, 512), "v": d["v"], **stored(*lists(rng)), **weights(rng, w)}
def setup_inputs_ends(rng):
    d = numbers_of(rng)
    o, e, h = rng.permutation(N) % 4, rng.permutation(N) % 4, rng.permutation(8)
    s = rng.choice([-1.0, 1.0], (N, 128, C, 4))
    s[o == 0] = -1
    s[o == 1] = rng.choice([-1.0, 1.0], (N, 1, C, 1))[o == 1]
    x = s * (0.955 + 0.02 * rng.random((N, 128, C, 4))) * 2.0 ** 30
    x[o == 3] = 2.0 ** -30
    size = np.where(o == 3, 2.0 ** -30, 2.0 ** 30)
    a = np.stack([rng.permutation(8) % 2 * 2.0 - 1.0 for r in range(N)]) * size[:, None]
    u = d["u"].reshape(N, 128, 128, 4)
    u[:, :, ::16] = a.astype(np.float32).astype(BF)[:, None, :, None]
    v = rng.choice([-1.0, 1.0], (N, 128, 512)) * np.where(o % 2 == 0, 2.0 ** 30, 2.0 ** -30)[:, None, None]
    q, m = lists(rng)
    c = np.arange(C)
    q[e == 0], m[e == 0] = c, C - 1 - c
    q[e == 1], m[e == 1] = C - 1 - c, c ^ 1
    q[e == 2], m[e == 2] = (c + 1) % C, (c + HALF) % C
    w = no_layers()
    i = np.arange(16)
    for r in range(N):
        for b in range(4):
            if o[r] < 3:
                for g in h[:3]: w[r, g, i, b, g, i, b] = -0.125
            w[r, h[4], i, b, h[3], i, b] = 2.0 ** 30 if o[r] == 3 else 2.0 ** -30
    return {"x": x.astype(np.float32).reshape(N, 128, 4 * C).astype(BF), "u": u.reshape(N, 128, 512), "v": v.astype(np.float32).astype(BF), **stored(q, m), **weights(rng, w)}
def setup_inputs_spread(rng):
    d = setup_inputs(rng)
    d["x"] = big(wide(rng, N, 128, 4 * C, cols=6))
    return d
def check_inputs(d):
    b = []
    for k in ("x", "u", "v"):
        a = np.abs(d[k].astype(np.float32))
        if not (np.isfinite(a).all() and ((a == 0) | (a >= 2.0 ** -30) & (a <= 2.0 ** 30)).all()): b.append("a value of " + k)
    none, least, most = [emit(mx_ref.quantize(np.full((128, 16), k, np.float32).astype(BF)))[1][0, 0] for k in (0.0, 2.0 ** -30, 2.0 ** 30)]
    c = np.arange(C)
    for r in range(N):
        if not (np.sort(gentries(d["gq"][r]), axis=1) == c).all(): b.append("gq: not each column once in a group")
        m = gentries(d["gm"][r])
        if not ((m >= 0) & (m < C)).all(): b.append("an entry of gm")
        elif not ((np.take_along_axis(m, m, axis=1) == c) & (m != c)).all(): b.append("gm: not pairs")
        if ((d["wc"][r] == 0x7F) | (d["wc"][r] == 0xFF)).any(): b.append("wc: a code that is no number")
        s = mx_ref.live(d["ws"][r])
        if ((s != none) & ((s < least) | (s > most))).any(): b.append("ws: a scale out of range")
        if (((d["wc"][r].reshape(16, 8, 512, 4) & 0x7F) != 0) & (s == none)[:, None, :, None]).any(): b.append("wc: a code other than zero under the scale of zeros")
    return b
def exchange(s, m):
    bit = np.roll(s[::16] > 0, 1, axis=0)
    return np.where(np.take_along_axis(bit, np.minimum(m, np.arange(C)), axis=1), m, np.arange(C))
def reference(x, u, v, gq, gm, wc, ws):
    qu = [mx_ref.quantize(u[r]) for r in range(N)]
    lay = [pk(wc[r], ws[r]) for r in range(N)]
    kept, pair = [gentries(gq[r]) for r in range(N)], [gentries(gm[r]) for r in range(N)]
    now = [x[r] for r in range(N)]
    for step in STEP:
        mid, back, sent = [], [], []
        for r in range(N):
            q, m = kept[r], pair[r]
            a, b = np.zeros((9, C), np.int64), np.zeros((9, C), np.int64)
            go = exchange(mx_ref.matmul(qu[r], mx_ref.quantize(now[r])), m)
            a[0] = np.arange(C)
            for g in range(8): a[g + 1] = q[g][go[g][a[g]]]
            t = ((now[r].astype(np.float32) + gcols(now[r], a[1:]).astype(np.float32)) * np.float32(0.5)).astype(BF)
            qt = mx_ref.quantize(t)
            go = exchange(mx_ref.matmul(qu[r], qt), m)
            inv = np.argsort(q, axis=1)
            b[8] = a[8]
            for g in range(7, -1, -1): b[g] = go[g][inv[g][b[g + 1]]]
            sent.append(mx_ref.quantize(tile([mx_ref.matmul(pick(lay[r], np.arange(128 * k, 128 * k + 128)), qt) * np.float32(0.03125) for k in range(4)])))
            miss = np.take_along_axis(a[:8] != b[:8], np.minimum(m, np.arange(C)), axis=1)
            kept[r] = np.where(miss, np.take_along_axis(q, m, axis=1), q)
            mid.append(t)
            back.append(b[:8])
        now = [(mid[r].astype(np.float32) + gcols(decode(sent[r ^ step]).astype(BF), back[r]).astype(np.float32)).astype(BF) for r in range(N)]
    y, qo = np.zeros((N, 128, C), np.float32), np.zeros((N, 8, C), np.float32)
    oc, osc = np.zeros((N, 128, 4 * C), np.uint8), np.zeros((N, 16, C), np.uint8)
    for r in range(N):
        q = mx_ref.quantize(now[r])
        y[r] = mx_ref.matmul(mx_ref.quantize(v[r]), q)
        qo[r] = kept[r]
        oc[r], osc[r] = emit(q)
    return {"y": y, "qo": qo, "oc": oc, "osc": osc}

@@ -1,0 +1,538 @@
+from concourse.bass import DstId, RemoteDMATransfer
+from concourse.mybir import dt, AluOpType, ActivationFunctionType
+
+C, N = 320, 8
+STEP = [4, 1, 2]
+OP, AF = AluOpType, ActivationFunctionType
+
+SCRATCH = {}
+SEMAPHORES = ["cv", "cs", "ct", "cg", "sent", "rarrq", "rarrs", "rsent"]
+
+
+def _declare():
+    def sb(name, n, d):
+        SCRATCH[name] = ("sbuf", [128, n], d)
+
+    def mx(name, n):
+        sb(name + "q", n, "float8_e4m3fn_x4")
+        sb(name + "s", n, "uint8")
+    for r in range(4):
+        mx("xm%d" % r, C)
+    for r in range(3):
+        mx("vm%d" % r, C)
+        mx("hm%d" % r, C)
+        mx("land%d" % r, C)
+        SEMAPHORES.extend(["arr%d" % r, "a8s%d" % r, "ashs%d" % r])
+    mx("rel", 160)
+    mx("um", 128)
+    mx("u2", 128)
+    mx("vw", 128)
+    mx("wm", 512)
+    mx("cm", 256)
+    mx("em", 512)
+    mx("lm", 128)
+    for n in ("ut", "vt", "cpat", "ones", "tl"):
+        sb(n, 512, "bfloat16")
+    sb("ct", 1024, "bfloat16")
+    sb("et", 2048, "bfloat16")
+    for n in ("blk", "wmask", "ar", "mr", "n0", "phi0", "phi1", "ee", "pho", "phb", "sg", "tin", "ash", "ta"):
+        sb(n, C, "bfloat16")
+    for n in ("ra", "rb"):
+        sb(n, 2 * C, "bfloat16")
+    for n in ("wr0", "wr1", "wr2", "wra", "wrb", "tb"):
+        sb(n, 352, "bfloat16")
+    sb("xh", 4 * C, "bfloat16")
+    sb("dsb", 4 * C, "bfloat16")
+    for n in ("rep1", "rep2"):
+        sb(n, 320, "bfloat16")
+    for n in ("z1", "z2"):
+        sb(n, 40, "bfloat16")
+    sb("kb", 20, "bfloat16")
+    sb("own", 24, "float32")
+    for n in ("hso", "mso", "hsb", "msb", "dd", "sm", "ft", "ff"):
+        sb(n, 160, "float32")
+    for n in ("w16", "wi", "gmf", "kap", "wf"):
+        sb(n, 20, "float32")
+    for n in ("amb", "b160", "t1", "qf", "yt"):
+        sb(n, C, "float32")
+    sb("cols", 16, "float32")
+    for n in ("gqi", "gmi"):
+        sb(n, 20, "int32")
+    for n in ("x0", "x1", "x2", "vv", "hh", "xi"):
+        sb(n, 4 * C, "bfloat16")
+    sb("ints", 24, "int32")
+    sb("ul", 8, "uint16")
+    for n in ("ql", "ml", "kn", "kxo", "kxb", "aoff", "boff", "a8", "n0l"):
+        sb(n, 20, "uint16")
+    sb("off", 160, "uint16")
+    for n in ("zd1", "zd2"):
+        SCRATCH[n] = ("dram", [16, 2, 160], "bfloat16")
+    for k in (0, 1, 2, 4, 5, 6, 7):
+        SCRATCH["ps%d" % k] = ("psum", [128, 512], "float32")
+    SEMAPHORES.extend(["dq", "dm", "dx", "du", "dw", "dv", "zw1", "zr1", "zw2", "zr2", "oend"])
+
+
+_declare()
+
+
+def _relays(topo, src, dst):
+    if topo.may_write(src, dst):
+        return []
+    c = [k for k in topo.cores_of(src) if k != src and topo.may_write(k, dst)]
+    same = [k for k in c if topo.die(k) == topo.die(src)]
+    other = [k for k in c if topo.die(k) != topo.die(src)]
+    return [same[0], other[0]]
+
+
+def _count(mask):
+    return bin(mask).count("1")
+
+
+def V(name, lo, hi, step=1, p0=0, p1=128):
+    return (name, lo, hi, step, p0, p1)
+
+
+def _machine(g, T):
+    eng = {"v": g.vector, "s": g.scalar, "t": g.tensor, "g": g, "y": g.sync}
+    cnt, log, snap, closed = {}, {}, {}, set()
+    known = {q: {} for q in eng}
+
+    def ap(r):
+        n, lo, hi, st, p0, p1 = r
+        if st == 1:
+            return T[n][p0:p1, lo:hi]
+        return T[n][p0:p1, lo:hi:st]
+
+    def hit(a, b):
+        if a[1] >= b[2] or b[1] >= a[2] or a[4] >= b[5] or b[4] >= a[5]:
+            return False
+        if a[3] == b[3] and a[3] > 1 and (a[1] - b[1]) % a[3]:
+            return False
+        return True
+
+    def learn(q, sem, c):
+        k = known[q]
+        if k.get(sem, 0) >= c:
+            return
+        k[sem] = c
+        for s, v in snap.get((sem, c), {}).items():
+            if k.get(s, 0) < v:
+                k[s] = v
+
+    def wait(q, sem, c):
+        if known[q].get(sem, 0) >= c:
+            return
+        if sem not in ("cv", "cs", "ct", "cg"):
+            c = cnt[sem]
+            closed.add(sem)
+        eng[q].wait_ge(T.sem[sem], c)
+        learn(q, sem, c)
+
+    def norm(r):
+        if r[0].startswith("ps"):
+            return (r[0], 0, 512, 1, 0, 128)
+        return r
+
+    def deps(q, reads, writes):
+        need = {}
+        for rs, w in ((reads, False), (writes, True)):
+            for r in rs:
+                r = norm(r)
+                ps = r[0].startswith("ps")
+                for (o, ow, oq, sem, c) in log.get(r[0], []):
+                    if (w or ow or (ps and oq != q)) and hit(r, o):
+                        if need.get(sem, 0) < c:
+                            need[sem] = c
+        own = known[q]
+        for sem in sorted(need, key=lambda s: (s == "c" + q, s)):
+            if own.get(sem, 0) < need[sem]:
+                wait(q, sem, need[sem])
+
+    def note(q, reads, writes, sem):
+        c = cnt[sem]
+        s = dict(known[q])
+        snap[(sem, c)] = s
+        for rs, w in ((reads, False), (writes, True)):
+            for r in rs:
+                r = norm(r)
+                old = log.get(r[0], [])
+                if w:
+                    old = [e for e in old if not (r[1] <= e[0][1] and e[0][2] <= r[2] and r[3] == 1
+                                                  and r[4] <= e[0][4] and e[0][5] <= r[5])]
+                log[r[0]] = old + [(r, w, q, sem, c)]
+
+    def op(q, fn, reads, writes):
+        deps(q, reads, writes)
+        sem = "c" + q
+        cnt[sem] = cnt.get(sem, 0) + 1
+        fn().then_inc(T.sem[sem], 1)
+        note(q, reads, writes, sem)
+
+    def dma(q, sem, out, inn, reads, writes):
+        deps(q, reads, writes)
+        if sem in closed:
+            raise ValueError("semaphore " + sem + " was waited for already")
+        cnt[sem] = cnt.get(sem, 0) + 16
+        eng[q].dma_start(out, inn).then_inc(T.sem[sem], 16)
+        note(q, reads, writes, sem)
+
+    def arrived(q, sem, c, writes):
+        cnt[sem] = c
+        wait(q, sem, c)
+
+    def finish():
+        for sem in sorted(cnt):
+            if known["g"].get(sem, 0) < cnt[sem]:
+                g.wait_ge(T.sem[sem], cnt[sem])
+
+    return {"ap": ap, "op": op, "dma": dma, "deps": deps, "arrived": arrived, "finish": finish, "cnt": cnt, "note": note}
+
+
+def _relay_program(g, core, T, topo):
+    for r in range(N):
+        src, dst = T.cores[r], T.cores[r ^ STEP[1]]
+        way = _relays(topo, src, dst)
+        if core not in way:
+            continue
+        i = way.index(core)
+        a, b = 160 * i, 160 * i + 160
+        rid, pid = topo.addr(dst, core)
+        m, e = topo.mask(core, dst), len(topo.engines(src, core)) // len(way)
+        g.wait_ge(T.sem.rarrq, e)
+        g.remote_dma(T.land1q[:, a:b].bitcast(dt.uint8), T.relq[:, 0:160].bitcast(dt.uint8), T.sem.arr1, T.sem.rsent, pid, rid, m)
+        g.wait_ge(T.sem.rarrs, e)
+        g.remote_dma(T.land1s[:, a:b], T.rels[:, 0:160], T.sem.arr1, T.sem.rsent, pid, rid, m)
+        g.wait_ge(T.sem.rsent, 2 * _count(m))
+
+
+def rank_program(g, core, T, topo):
+    rank = T.rank_of(core)
+    if rank is None:
+        _relay_program(g, core, T, topo)
+        return
+    M = _machine(g, T)
+    ap, op, dma = M["ap"], M["op"], M["dma"]
+
+    def src(inn, off):
+        return ap(inn) if off is None else ap(inn).indirect(ap(off))
+
+    def rd(*rs):
+        return [r for r in rs if isinstance(r, tuple)]
+
+    def cp(out, inn, off=None):
+        op("v", lambda: g.vector.tensor_copy(ap(out), src(inn, off)), rd(inn, off), [out])
+
+    def tt(out, a, b, o, off=None):
+        op("v", lambda: g.vector.tensor_tensor(ap(out), src(a, off), ap(b), o), rd(a, b, off), [out])
+
+    def ts(out, a, s1, s2, o0, o1=None, off=None):
+        k1 = ap(s1) if isinstance(s1, tuple) else s1
+        k2 = ap(s2) if isinstance(s2, tuple) else s2
+        if o1 is None:
+            op("v", lambda: g.vector.tensor_scalar(ap(out), src(a, off), k1, None, o0), rd(a, s1, off), [out])
+        else:
+            op("v", lambda: g.vector.tensor_scalar(ap(out), src(a, off), k1, k2, o0, o1), rd(a, s1, s2, off), [out])
+
+    def act(out, inn, func=AF.Copy, scale=1.0, bias=None, off=None):
+        k = ap(scale) if isinstance(scale, tuple) else scale
+        if bias is None:
+            op("s", lambda: g.scalar.activation(ap(out), src(inn, off), func, scale=k), rd(inn, scale, off), [out])
+        else:
+            op("s", lambda: g.scalar.activation(ap(out), src(inn, off), func, bias=ap(bias), scale=k), rd(inn, scale, bias, off), [out])
+
+    def fill(r, c):
+        op("v", lambda: g.vector.memset(ap(r), c), [], [r])
+
+    def tr(out, inn):
+        op("v", lambda: g.vector.transpose(ap(out), ap(inn)), [inn], [out])
+
+    def qz(n, lo, hi, inn):
+        q, s = V(n + "q", lo, hi), V(n + "s", lo, hi)
+        op("v", lambda: g.vector.quantize_mx(ap(q), ap(s), ap(inn)), [inn], [q, s])
+
+    def mm(ps, n, a, alo, b, blo=0):
+        aq, as_, bq, bs = V(a + "q", alo, alo + 128), V(a + "s", alo, alo + 128), V(b + "q", blo, blo + n), V(b + "s", blo, blo + n)
+        o = V(ps, 0, n)
+        op("t", lambda: g.tensor.matmul_mx(ap(o), ap(aq), ap(as_), ap(bq), ap(bs), True, True), [aq, as_, bq, bs], [o])
+
+    def iota(r, pattern, base, cm, f=True):
+        if f:
+            op("g", lambda: g.iota(ap(r), pattern, base, cm, allow_small_or_imprecise_dtypes=True), [], [r])
+        else:
+            op("g", lambda: g.iota(ap(r), pattern, base, cm), [], [r])
+
+    def sel(out, inn, pattern, o, base, cm):
+        op("g", lambda: g.affine_select(ap(out), ap(inn), pattern, o, 0.0, base, cm), [inn], [out])
+
+    dma("y", "dq", T.gqi[:], T.gq[:], [], [V("gqi", 0, 20)])
+    dma("s", "dm", T.gmi[:], T.gm[:], [], [V("gmi", 0, 20)])
+    dma("s", "du", T.ut[:], T.u[:], [], [V("ut", 0, 512)])
+    dma("y", "dx", T.x0[:], T.x[:], [], [V("x0", 0, 4 * C)])
+    dma("y", "dw", T.wmq[:, 0:512].bitcast(dt.uint8), T.wc[:, 0:2048], [], [V("wmq", 0, 512)])
+    dma("y", "dw", T.wms[:, 0:512], T.ws[:, 0:512], [], [V("wms", 0, 512)])
+    dma("y", "dv", T.vt[:], T.v[:], [], [V("vt", 0, 512)])
+    IDENT = V("ra", 0, C)
+    pid, l16i, a4i, l32i = [V("ints", k, k + 1) for k in range(4)]
+    iota(pid, [[1, 1]], 0, 1, False)
+    iota(IDENT, [[1, C]], -160, 0)
+    iota(V("blk", 0, C), [[0, 10], [1, 2], [0, 16]], 0, 0)
+    iota(V("w16", 0, 20), [[16, 20]], 0, 0)
+    iota(V("ints", 8, 16), [[16, 8]], 112, 0, False)
+
+    def col(k):
+        return V("cols", k, k + 1)
+    L16, A4, L32, L32B, MT, MT2, MTN, KE, KO, C1, C0 = [col(k) for k in range(11)]
+    ts(l16i, pid, 15, None, OP.bitwise_and)
+    ts(a4i, pid, 3, 12, OP.arith_shift_right, OP.bitwise_and)
+    ts(l32i, pid, 31, None, OP.bitwise_and)
+    cp(L16, l16i)
+    cp(A4, a4i)
+    cp(L32, l32i)
+    ts(KE, L16, 1.0, None, OP.is_equal)
+    ts(KO, L16, 2.0, None, OP.is_equal)
+    tt(MT, L16, A4, OP.is_equal)
+    tt(C1, KO, KE, OP.subtract)
+    ts(C0, KO, -1.0, 1.0, OP.mult, OP.add)
+    fill(V("own", 8, 16), 320.0)
+    sel(V("own", 16, 24), V("own", 8, 16), [[-16, 8]], OP.is_ge, 0, 1)
+    sel(V("own", 0, 8), V("own", 16, 24), [[16, 8]], OP.is_ge, 15, -1)
+    iota(V("cpat", 0, 512), [[0, 8], [1, 16], [64, 4]], 0, 0)
+    fill(V("ones", 0, 512), 1.0)
+    fill(V("phi0", 0, C), 1.0)
+    fill(V("tl", 320, 512), 0.0)
+    act(V("wmask", 0, C), V("blk", 0, C), AF.Identity, C1, C0)
+    act(V("ra", C, 2 * C), IDENT)
+    act(V("rb", C, 2 * C), IDENT)
+    for n in ("wr0", "wr1", "wr2", "wra", "wrb"):
+        fill(V(n, 0, 16), 0.0)
+        fill(V(n, 336, 352), 0.0)
+    QL, ML, KN, KXO, KXB = [V(n, 0, 20) for n in ("ql", "ml", "kn", "kxo", "kxb")]
+    WM = V("wmask", 0, C)
+    cp(QL, V("gqi", 0, 20))
+    cp(ML, V("gmi", 0, 20))
+    cp(V("ar", 0, C), IDENT, QL)
+    act(V("mr", 0, C), IDENT, AF.Copy, 1.0, None, ML)
+    ts(V("z1", 0, 20), V("gqi", 0, 20), -160.0, None, OP.add)
+    tt(V("wr0", 16, 336), V("ar", 0, C), WM, OP.mult, ML)
+
+    def turn(n):
+        tr(V("ta", 0, C), V(n, 16, 336))
+        tr(V("tb", 0, 352), V(n, 0, 352))
+
+    def entries(out, lo):
+        tt(V(out, lo, lo + 20, 2), V("ta", 1, C, 32), V("tb", 17, C, 32), OP.add)
+        tt(V(out, lo + 1, lo + 20, 2), V("ta", 18, C, 32), V("tb", 34, 352, 32), OP.add)
+
+    def spread(z, zd, rep, w, rdsem):
+        for k in range(8):
+            dma("y", w, T[zd][:, :, 20 * k:20 * k + 20], T[z][16 * k:16 * k + 16, 0:40], [V(z, 0, 40, 1, 16 * k, 16 * k + 16)],
+                [V(zd, 40 * k, 40 * k + 40)])
+        for k in range(8):
+            dma("y", rdsem, T[rep][16 * k:16 * k + 16, 0:320], T[zd][:, :, :], [V(zd, 0, 320)], [V(rep, 0, 320, 1, 16 * k, 16 * k + 16)])
+
+    turn("wr0")
+    entries("z1", 20)
+    spread("z1", "zd1", "rep1", "zw1", "zr1")
+    ts(V("ints", 16, 24), V("ints", 8, 16), 127, None, OP.bitwise_and)
+    cp(V("ul", 0, 8), V("ints", 16, 24))
+    qz("um", 0, 128, V("ut", 0, 512))
+    op("v", lambda: g.vector.tensor_copy(T.u2q[:, 0:128].bitcast(dt.uint32), T.umq[:, 0:128].bitcast(dt.uint32).indirect(T.ul[:, 0:8])),
+       [V("umq", 0, 128), V("ul", 0, 8)], [V("u2q", 0, 128)])
+    op("s", lambda: g.scalar.activation(T.u2s[:, 0:128], T.ums[:, 0:128].indirect(T.ul[:, 0:8]), AF.Copy),
+       [V("ums", 0, 128), V("ul", 0, 8)], [V("u2s", 0, 128)])
+    qz("xm0", 0, C, V("x0", 0, 4 * C))
+    mm("ps0", C, "u2", 0, "xm0")
+    cp(V("gmf", 0, 20), V("gmi", 0, 20))
+    ts(V("wi", 0, 20), V("w16", 0, 20), L16, None, OP.add)
+    tt(V("kap", 0, 20), V("gmf", 0, 20), V("wi", 0, 20), OP.min)
+    cp(V("kxo", 0, 20, 2), V("kap", 0, 10))
+    cp(V("kxo", 1, 20, 2), V("kap", 10, 20))
+    ts(MT2, MT, 2.0, None, OP.mult)
+    ts(MTN, MT, -1.0, None, OP.mult)
+    act(V("pho", 0, C), V("phi0", 0, C), AF.Copy, MT)
+    act(V("phb", 0, C), V("phi0", 0, C), AF.Copy, MT)
+    ts(L32B, L32, -16.0, None, OP.add)
+    ts(V("ct", 0, 512), V("cpat", 0, 512), L32, None, OP.is_equal)
+    ts(V("ct", 512, 1024), V("cpat", 0, 512), L32B, None, OP.is_equal)
+    qz("cm", 0, 256, V("ct", 0, 1024))
+
+    def halves(X):
+        for b in range(4):
+            act(V("xh", C * b, C * b + C), V(X, b, 4 * C, 4), AF.Copy, 0.5)
+        act(V("xi", 0, 4 * C), V(X, 0, 4 * C), AF.Copy, 0.5)
+    halves("x0")
+
+    def differ(rep):
+        A, B = V(rep, 0, 160), V(rep, 160, 320)
+        tt(V("dd", 0, 160), B, A, OP.subtract)
+        tt(V("sm", 0, 160), B, A, OP.add)
+
+    def tables(H, W):
+        for k in range(8):
+            o = 4 * (k % 2) + k // 2
+            act(V(H, o, 160, 8), V("dd", 20 * k, 20 * k + 20))
+            act(V(W, o, 160, 8), V("sm", 20 * k, 20 * k + 20), AF.Identity, 0.5, V("own", k, k + 1))
+
+    def bits(kx, phi):
+        ts(V("sg", 0, C), V("ps0", 0, C), 0.0, 0.5, OP.is_gt, OP.subtract)
+        tt(V("tin", 0, C), V("sg", 0, C), V(phi, 0, C), OP.mult, kx)
+        tr(V("tl", 0, C), V("tin", 0, C))
+        qz("lm", 0, 128, V("tl", 0, 512))
+        mm("ps1", 128, "cm", 0, "lm")
+        mm("ps2", 128, "cm", 128, "lm")
+
+    def places(H, W):
+        for h in range(2):
+            a, b = 80 * h, 80 * h + 80
+            tt(V("ft", a, b), V("ps%d" % (1 + h), 0, 80), V(H, a, b), OP.mult)
+        for h in range(2):
+            a, b = 80 * h, 80 * h + 80
+            tt(V("ff", a, b), V("ft", a, b), V(W, a, b), OP.add)
+
+    def listed(g_):
+        k = 4 * (g_ % 2) + g_ // 2
+        cp(V("off", 20 * g_, 20 * g_ + 20), V("ff", k, 160, 8))
+
+    def step(a, b, g_):
+        o = 20 * g_
+        act(V(b, 160, 320), V(a, 0, 2 * C), AF.Copy, 1.0, None, V("off", o + 10, o + 20))
+        cp(V(b, 0, 160), V(a, 0, 2 * C), V("off", o, o + 10))
+
+    bits(KXO, "pho")
+    for b in range(4):
+        sel(V("et", 512 * b, 512 * b + 512), V("ones", 0, 512), [[1, 128], [1000, 4]], OP.is_equal, -1000 * b, -1)
+    op("v", lambda: g.vector.tensor_copy(T.n0[:, 0:C].indirect(T.ql[:, 0:20]), ap(IDENT)), [IDENT, QL], [V("n0", 0, C)])
+    ts(V("own", 0, 8), V("own", 0, 8), 160.0, None, OP.add)
+    differ("rep1")
+    tables("hso", "mso")
+    tt(V("wr1", 16, 336), V("n0", 0, C), WM, OP.mult)
+    turn("wr1")
+    entries("z2", 0)
+    ts(V("n0l", 0, 20), V("z2", 0, 20), 160.0, None, OP.add)
+    tt(V("wr2", 16, 336), V("mr", 0, C), WM, OP.mult, V("n0l", 0, 20))
+    turn("wr2")
+    entries("z2", 20)
+    spread("z2", "zd2", "rep2", "zw2", "zr2")
+
+    for rnd in range(3):
+        Y, VV, HH = "x%d" % (1 + rnd % 2), "vv", "hh"
+        vm, hm, land = "vm%d" % rnd, "hm%d" % rnd, "land%d" % rnd
+        partner = T.cores[rank ^ STEP[rnd]]
+        if rnd:
+            bits(KXO, "pho")
+        places("hso", "mso")
+        cur, nxt = "ra", "rb"
+        listed(7)
+        listed(6)
+        for g_ in range(7, 0, -1):
+            step(cur, nxt, g_)
+            if g_ > 1:
+                listed(g_ - 2)
+            cur, nxt = nxt, cur
+        tt(V("wra", 16, 336), V(cur, 0, 2 * C), WM, OP.mult, V("off", 0, 20))
+        turn("wra")
+        entries("wf", 0)
+        ts(V("aoff", 0, 20), V("wf", 0, 20), 160.0, None, OP.add)
+        for b in range(4):
+            tt(V(VV, b, 4 * C, 4), V("xh", C * b, C * b + C), V("xi", b, 4 * C, 4), OP.add, V("aoff", 0, 20))
+        for k in range(8):
+            dma("y", "a8s%d" % rnd, T.a8[16 * k:16 * k + 16, 0:20], T.aoff[112:128, 0:20], [V("aoff", 0, 20, 1, 112, 128)],
+                [V("a8", 0, 20, 1, 16 * k, 16 * k + 16)])
+        dma("y", "ashs%d" % rnd, T.ash[16:128, 0:C], T.wra[0:112, 16:336], [V("wra", 16, 336, 1, 0, 112)], [V("ash", 0, C, 1, 16, 128)])
+        qz(vm, 0, C, V(VV, 0, 4 * C))
+        mm("ps0", C, "u2", 0, vm)
+        if rnd == 0:
+            differ("rep2")
+            tables("hsb", "msb")
+        for b in range(4):
+            mm("ps%d" % (4 + b), C, "wm", 128 * b, vm)
+            act(V(HH, b, 4 * C, 4), V("ps%d" % (4 + b), 0, C), AF.Copy, 0.03125)
+        if rnd == 0:
+            tt(V("kb", 0, 20), V("z2", 0, 20), V("z2", 20, 40), OP.min)
+            ts(V("kxb", 0, 20, 2), V("kb", 0, 10), 160.0, None, OP.add)
+            ts(V("kxb", 1, 20, 2), V("kb", 10, 20), 160.0, None, OP.add)
+            cp(V("ash", 0, C, 1, 0, 16), V("rb", C, 2 * C, 1, 0, 16))
+        bits(KXB, "phb")
+        if rnd == 0:
+            qz("em", 0, 512, V("et", 0, 2048))
+            qz("vw", 0, 128, V("vt", 0, 512))
+        places("hsb", "msb")
+        cur, nxt = "ra", "rb"
+        listed(0)
+        listed(1)
+        for g_ in range(8):
+            step(cur, nxt, g_)
+            if g_ == 0:
+                qz(hm, 0, C, V(HH, 0, 4 * C))
+            if g_ < 6:
+                listed(g_ + 2)
+            if g_ == 0:
+                M["deps"]("g", [V(hm + "q", 0, C), V(hm + "s", 0, C)], [])
+                hq, hs, lq, ls = T[hm + "q"], T[hm + "s"], T[land + "q"], T[land + "s"]
+                way = _relays(topo, core, partner)
+                tot = 0
+                if not way:
+                    rid, p = topo.addr(partner, core)
+                    m = topo.mask(core, partner)
+                    g.remote_dma(lq[:, 0:C].bitcast(dt.uint8), hq[:, 0:C].bitcast(dt.uint8), T.sem["arr%d" % rnd], T.sem.sent, p, rid, m)
+                    g.remote_dma(ls[:, 0:C], hs[:, 0:C], T.sem["arr%d" % rnd], T.sem.sent, p, rid, m)
+                    tot, got = 2 * _count(m), 2 * _count(m)
+                else:
+                    got, fq, fs = 0, [], []
+                    for i, k in enumerate(way):
+                        a, b = 160 * i, 160 * i + 160
+                        rid, p = topo.addr(k, core)
+                        e = topo.engines(core, k)
+                        n = len(e) // len(way)
+                        m = sum(1 << x for x in e[n * i:n * i + n])
+                        to = [DstId(rid=rid, pnc=p)]
+                        fq.append(RemoteDMATransfer(dst_ids=to, dma_engine_mask=m, remote_sem=T.sem.rarrq,
+                                                    src=hq[:, a:b].bitcast(dt.uint8), dst=T.relq[:, 0:160].bitcast(dt.uint8)))
+                        fs.append(RemoteDMATransfer(dst_ids=to, dma_engine_mask=m, remote_sem=T.sem.rarrs,
+                                                    src=hs[:, a:b], dst=T.rels[:, 0:160]))
+                        tot += 2 * n
+                    g.remote_dma_fused(fq, local_sem=T.sem.sent)
+                    g.remote_dma_fused(fs, local_sem=T.sem.sent)
+                    for k in _relays(topo, partner, core):
+                        got += 2 * _count(topo.mask(k, core))
+                M["cnt"]["sent"] = M["cnt"].get("sent", 0) + tot
+            cur, nxt = nxt, cur
+        tt(V("wrb", 16, 336), V(cur, 0, C), WM, OP.mult, V("a8", 0, 20))
+        turn("wrb")
+        entries("wf", 0)
+        ts(V("boff", 0, 20), V("wf", 0, 20), 160.0, None, OP.add)
+        M["arrived"]("t", "arr%d" % rnd, got, [])
+        for b in range(4):
+            mm("ps%d" % (4 + b), C, "em", 128 * b, land)
+            act(V("dsb", C * b, C * b + C), V("ps%d" % (4 + b), 0, C))
+        ph, pn = ("phi0", "phi1") if rnd % 2 == 0 else ("phi1", "phi0")
+        tt(V("ee", 0, C), V("wrb", 16, 336), V("ash", 0, C), OP.is_equal)
+
+        def new(b):
+            tt(V(Y, b, 4 * C, 4), V("dsb", C * b, C * b + C), V(VV, b, 4 * C, 4), OP.add, V("boff", 0, 20))
+        new(0)
+        tt(V(pn, 0, C), V(ph, 0, C), V("ee", 0, C), OP.is_equal)
+        new(1)
+        if rnd < 2:
+            act(V("pho", 0, C), V(pn, 0, C), AF.Identity, MT2, MTN, KXO)
+            act(V("phb", 0, C), V(pn, 0, C), AF.Identity, MT2, MTN, KXB)
+        new(2)
+        new(3)
+        qz("xm%d" % (rnd + 1), 0, C, V(Y, 0, 4 * C))
+        if rnd < 2:
+            mm("ps0", C, "u2", 0, "xm%d" % (rnd + 1))
+            halves(Y)
+        else:
+            mm("ps0", C, "vw", 0, "xm3")
+            dma("y", "oend", T.oc[:, 0:4 * C], T.xm3q[:, 0:C].bitcast(dt.uint8), [V("xm3q", 0, C)], [])
+            act(V("yt", 0, C), V("ps0", 0, C))
+            dma("s", "oend", T.y[:], T.yt[:], [V("yt", 0, C)], [])
+            for k in range(4):
+                dma("y", "oend", T.osc[4 * k:4 * k + 4, 0:C], T.xm3s[32 * k:32 * k + 4, 0:C], [V("xm3s", 0, C)], [])
+            cp(KN, V("kap", 0, 20))
+            tt(V("amb", 0, C), V("ar", 0, C), V("wr0", 16, 336), OP.subtract)
+            tt(V("t1", 0, C), V(pn, 0, C), V("amb", 0, C), OP.mult, KN)
+            ts(V("b160", 0, C), V("wr0", 16, 336), 160.0, None, OP.add)
+            tt(V("qf", 0, C), V("t1", 0, C), V("b160", 0, C), OP.add)
+            dma("y", "oend", T.qo[:], T.qf[0:128:16, 0:C], [V("qf", 0, C)], [])
+    M["finish"]()

@@ -3,10 +3,13 @@ from concourse.mybir import dt, AluOpType, ActivationFunctionType
 
 C, N = 320, 8
 STEP = [4, 1, 2]
+PARTS = [(0, 192), (192, 320)]
+PAD = 16
+PADDED = ("ar", "br", "mn", "tin", "wra", "wrb", "ee2", "cum")
 OP, AF = AluOpType, ActivationFunctionType
 
 SCRATCH = {}
-SEMAPHORES = ["cv", "cs", "ct", "cg", "sent", "rarrq", "rarrs", "rsent"]
+SEMAPHORES = ["cv", "cs", "ct", "cg", "sent", "rarr", "rsent", "dq", "dm", "dx", "du", "dw", "dv", "oend"]
 
 
 def _declare():
@@ -16,60 +19,52 @@ def _declare():
     def mx(name, n):
         sb(name + "q", n, "float8_e4m3fn_x4")
         sb(name + "s", n, "uint8")
-    for r in range(4):
-        mx("xm%d" % r, C)
+    mx("xm", C)
+    mx("vm", C)
     for r in range(3):
-        mx("vm%d" % r, C)
         mx("hm%d" % r, C)
         mx("land%d" % r, C)
         SEMAPHORES.extend(["arr%d" % r, "a8s%d" % r, "ashs%d" % r])
-    mx("rel", 160)
+    mx("rel", C)
     mx("um", 128)
     mx("u2", 128)
     mx("vw", 128)
     mx("wm", 512)
-    mx("cm", 256)
     mx("em", 512)
-    mx("lm", 128)
-    for n in ("ut", "vt", "cpat", "ones", "tl"):
+    for n in ("ut", "vt", "ones"):
         sb(n, 512, "bfloat16")
-    sb("ct", 1024, "bfloat16")
     sb("et", 2048, "bfloat16")
-    for n in ("blk", "wmask", "ar", "mr", "n0", "phi0", "phi1", "ee", "pho", "phb", "sg", "tin", "ash", "ta"):
+    for n in ("ident", "mr", "ee0", "ee1", "phb", "sg", "ash", "ak", "ra", "rb"):
         sb(n, C, "bfloat16")
-    for n in ("ra", "rb"):
-        sb(n, 2 * C, "bfloat16")
-    for n in ("wr0", "wr1", "wr2", "wra", "wrb", "tb"):
-        sb(n, 352, "bfloat16")
-    sb("xh", 4 * C, "bfloat16")
-    sb("dsb", 4 * C, "bfloat16")
-    for n in ("rep1", "rep2"):
-        sb(n, 320, "bfloat16")
-    for n in ("z1", "z2"):
-        sb(n, 40, "bfloat16")
-    sb("kb", 20, "bfloat16")
-    sb("own", 24, "float32")
-    for n in ("hso", "mso", "hsb", "msb", "dd", "sm", "ft", "ff"):
-        sb(n, 160, "float32")
-    for n in ("w16", "wi", "gmf", "kap", "wf"):
-        sb(n, 20, "float32")
-    for n in ("amb", "b160", "t1", "qf", "yt"):
+    for n in PADDED:
+        sb(n, C + 2 * PAD, "bfloat16")
+    sb("turned", 2 * C + 2 * PAD, "bfloat16")
+    for n in ("xh", "xi", "dsb", "x0", "x1", "x2", "vv", "hh"):
+        sb(n, 4 * C, "bfloat16")
+    for n in ("qf", "yt"):
         sb(n, C, "float32")
+    sb("i160", 160, "float32")
+    for n in ("za", "zc", "do", "ao", "db", "ab", "ft", "ff"):
+        sb(n, 64, "float32")
+    for n in ("w16", "wi", "we", "wo", "kap", "dm", "fw", "t20"):
+        sb(n, 20, "float32")
+    for n in ("c1w", "e2w", "n0w", "mnw"):
+        sb(n, 32, "float32")
     sb("cols", 16, "float32")
     for n in ("gqi", "gmi"):
         sb(n, 20, "int32")
-    for n in ("x0", "x1", "x2", "vv", "hh", "xi"):
-        sb(n, 4 * C, "bfloat16")
     sb("ints", 24, "int32")
     sb("ul", 8, "uint16")
-    for n in ("ql", "ml", "kn", "kxo", "kxb", "aoff", "boff", "a8", "n0l"):
+    for n in ("ql", "ml", "kn", "kxb", "a8", "qoff"):
         sb(n, 20, "uint16")
-    sb("off", 160, "uint16")
-    for n in ("zd1", "zd2"):
-        SCRATCH[n] = ("dram", [16, 2, 160], "bfloat16")
-    for k in (0, 1, 2, 4, 5, 6, 7):
+    for n in ("aoff", "boff", "n0l"):
+        sb(n, 32, "uint16")
+    for n in ("clo", "clb", "own"):
+        sb(n, 4, "uint16")
+    for n in ("offo", "offb"):
+        sb(n, 180, "uint16")
+    for k in range(6):
         SCRATCH["ps%d" % k] = ("psum", [128, 512], "float32")
-    SEMAPHORES.extend(["dq", "dm", "dx", "du", "dw", "dv", "zw1", "zr1", "zw2", "zr2", "oend"])
 
 
 _declare()
@@ -78,10 +73,10 @@ _declare()
 def _relays(topo, src, dst):
     if topo.may_write(src, dst):
         return []
-    c = [k for k in topo.cores_of(src) if k != src and topo.may_write(k, dst)]
+    c = [k for k in topo.cores_of(src) if topo.may_write(k, dst)]
     same = [k for k in c if topo.die(k) == topo.die(src)]
     other = [k for k in c if topo.die(k) != topo.die(src)]
-    return [same[0], other[0]]
+    return [same[0], other[0], same[1]]
 
 
 def _count(mask):
@@ -176,7 +171,7 @@ def _machine(g, T):
         eng[q].dma_start(out, inn).then_inc(T.sem[sem], 16)
         note(q, reads, writes, sem)
 
-    def arrived(q, sem, c, writes):
+    def arrived(q, sem, c):
         cnt[sem] = c
         wait(q, sem, c)
 
@@ -185,24 +180,28 @@ def _machine(g, T):
             if known["g"].get(sem, 0) < cnt[sem]:
                 g.wait_ge(T.sem[sem], cnt[sem])
 
-    return {"ap": ap, "op": op, "dma": dma, "deps": deps, "arrived": arrived, "finish": finish, "cnt": cnt, "note": note}
+    return {"ap": ap, "op": op, "dma": dma, "deps": deps, "arrived": arrived, "finish": finish, "cnt": cnt}
 
 
 def _relay_program(g, core, T, topo):
-    for r in range(N):
-        src, dst = T.cores[r], T.cores[r ^ STEP[1]]
-        way = _relays(topo, src, dst)
-        if core not in way:
-            continue
-        i = way.index(core)
-        a, b = 160 * i, 160 * i + 160
-        rid, pid = topo.addr(dst, core)
-        m, e = topo.mask(core, dst), len(topo.engines(src, core)) // len(way)
-        g.wait_ge(T.sem.rarrq, e)
-        g.remote_dma(T.land1q[:, a:b].bitcast(dt.uint8), T.relq[:, 0:160].bitcast(dt.uint8), T.sem.arr1, T.sem.rsent, pid, rid, m)
-        g.wait_ge(T.sem.rarrs, e)
-        g.remote_dma(T.land1s[:, a:b], T.rels[:, 0:160], T.sem.arr1, T.sem.rsent, pid, rid, m)
-        g.wait_ge(T.sem.rsent, 2 * _count(m))
+    for s in range(3):
+        for r in range(N):
+            src, dst = T.cores[r], T.cores[r ^ STEP[s]]
+            way = _relays(topo, src, dst)
+            if core not in way:
+                continue
+            i = way.index(core)
+            rid, pid = topo.addr(dst, core)
+            m, e = topo.mask(core, dst), _count(topo.mask(src, core))
+            lq, ls, arr = T["land%dq" % s], T["land%ds" % s], T.sem["arr%d" % s]
+            if i < 2:
+                a, b = C // 2 * i, C // 2 * (i + 1)
+                g.wait_ge(T.sem.rarr, e // 2)
+                g.remote_dma(lq[:, a:b].bitcast(dt.uint8), T.relq[:, a:b].bitcast(dt.uint8), arr, T.sem.rsent, pid, rid, m)
+            else:
+                g.wait_ge(T.sem.rarr, e)
+                g.remote_dma(ls[:, 0:C], T.rels[:, 0:C], arr, T.sem.rsent, pid, rid, m)
+            g.wait_ge(T.sem.rsent, _count(m))
 
 
 def rank_program(g, core, T, topo):
@@ -246,13 +245,12 @@ def rank_program(g, core, T, topo):
     def tr(out, inn):
         op("v", lambda: g.vector.transpose(ap(out), ap(inn)), [inn], [out])
 
-    def qz(n, lo, hi, inn):
-        q, s = V(n + "q", lo, hi), V(n + "s", lo, hi)
+    def qz(n, lo, hi, tile):
+        q, s, inn = V(n + "q", lo, hi), V(n + "s", lo, hi), V(tile, 4 * lo, 4 * hi)
         op("v", lambda: g.vector.quantize_mx(ap(q), ap(s), ap(inn)), [inn], [q, s])
 
-    def mm(ps, n, a, alo, b, blo=0):
-        aq, as_, bq, bs = V(a + "q", alo, alo + 128), V(a + "s", alo, alo + 128), V(b + "q", blo, blo + n), V(b + "s", blo, blo + n)
-        o = V(ps, 0, n)
+    def mm(ps, a, alo, b, lo, hi):
+        aq, as_, bq, bs, o = V(a + "q", alo, alo + 128), V(a + "s", alo, alo + 128), V(b + "q", lo, hi), V(b + "s", lo, hi), V(ps, 0, hi - lo)
         op("t", lambda: g.tensor.matmul_mx(ap(o), ap(aq), ap(as_), ap(bq), ap(bs), True, True), [aq, as_, bq, bs], [o])
 
     def iota(r, pattern, base, cm, f=True):
@@ -264,275 +262,273 @@ def rank_program(g, core, T, topo):
     def sel(out, inn, pattern, o, base, cm):
         op("g", lambda: g.affine_select(ap(out), ap(inn), pattern, o, 0.0, base, cm), [inn], [out])
 
-    dma("y", "dq", T.gqi[:], T.gq[:], [], [V("gqi", 0, 20)])
-    dma("s", "dm", T.gmi[:], T.gm[:], [], [V("gmi", 0, 20)])
-    dma("s", "du", T.ut[:], T.u[:], [], [V("ut", 0, 512)])
+    def R(n):
+        return V(n, PAD, PAD + C) if n in PADDED else V(n, 0, C)
+
+    def W(n):
+        return V(n, 0, 20)
+
+    L16, ODD, EVEN, H1, HH, HO, T1, C160 = [V("cols", k, k + 1) for k in range(8)]
+    TURNED = V("turned", 0, 2 * C + 2 * PAD)
+
+    def gather(out, win, off, o=0):
+        lo = R(out)[1]
+        act(V(out, lo + 160, lo + C), R(win), AF.Copy, 1.0, None, V(off, o + 10, o + 20))
+        cp(V(out, lo, lo + 160), R(win), V(off, o, o + 10))
+
+    def pads(n):
+        fill(V(n, 0, PAD), 0.0)
+        fill(V(n, PAD + C, 2 * PAD + C), 0.0)
+
+    def turn(row):
+        tr(V("turned", 0, C), R(row))
+        tr(V("turned", C, 2 * C + 2 * PAD), V(row, 0, C + 2 * PAD))
+
+    def entries(out, base):
+        ts(V(out, 0, 32), TURNED, base, None, OP.add, None, V("own", 0, 2))
+
+    dma("y", "dq", T.gqi[:], T.gq[:], [], [W("gqi")])
+    dma("s", "dm", T.gmi[:], T.gm[:], [], [W("gmi")])
     dma("y", "dx", T.x0[:], T.x[:], [], [V("x0", 0, 4 * C)])
+    dma("s", "du", T.ut[:], T.u[:], [], [V("ut", 0, 512)])
     dma("y", "dw", T.wmq[:, 0:512].bitcast(dt.uint8), T.wc[:, 0:2048], [], [V("wmq", 0, 512)])
     dma("y", "dw", T.wms[:, 0:512], T.ws[:, 0:512], [], [V("wms", 0, 512)])
     dma("y", "dv", T.vt[:], T.v[:], [], [V("vt", 0, 512)])
-    IDENT = V("ra", 0, C)
-    pid, l16i, a4i, l32i = [V("ints", k, k + 1) for k in range(4)]
+    IDENT = R("ident")
+    pid, i0, i1, i2 = [V("ints", k, k + 1) for k in range(4)]
     iota(pid, [[1, 1]], 0, 1, False)
+    iota(W("w16"), [[16, 20]], 0, 0)
     iota(IDENT, [[1, C]], -160, 0)
-    iota(V("blk", 0, C), [[0, 10], [1, 2], [0, 16]], 0, 0)
-    iota(V("w16", 0, 20), [[16, 20]], 0, 0)
+    iota(V("i160", 0, 160), [[0, 8], [16, 20]], 0, 0)
     iota(V("ints", 8, 16), [[16, 8]], 112, 0, False)
+    iota(V("ones", 0, 512), [[0, 512]], 1, 0)
 
-    def col(k):
-        return V("cols", k, k + 1)
-    L16, A4, L32, L32B, MT, MT2, MTN, KE, KO, C1, C0 = [col(k) for k in range(11)]
-    ts(l16i, pid, 15, None, OP.bitwise_and)
-    ts(a4i, pid, 3, 12, OP.arith_shift_right, OP.bitwise_and)
-    ts(l32i, pid, 31, None, OP.bitwise_and)
-    cp(L16, l16i)
-    cp(A4, a4i)
-    cp(L32, l32i)
-    ts(KE, L16, 1.0, None, OP.is_equal)
-    ts(KO, L16, 2.0, None, OP.is_equal)
-    tt(MT, L16, A4, OP.is_equal)
-    tt(C1, KO, KE, OP.subtract)
-    ts(C0, KO, -1.0, 1.0, OP.mult, OP.add)
-    fill(V("own", 8, 16), 320.0)
-    sel(V("own", 16, 24), V("own", 8, 16), [[-16, 8]], OP.is_ge, 0, 1)
-    sel(V("own", 0, 8), V("own", 16, 24), [[16, 8]], OP.is_ge, 15, -1)
-    iota(V("cpat", 0, 512), [[0, 8], [1, 16], [64, 4]], 0, 0)
-    fill(V("ones", 0, 512), 1.0)
-    fill(V("phi0", 0, C), 1.0)
-    fill(V("tl", 320, 512), 0.0)
-    act(V("wmask", 0, C), V("blk", 0, C), AF.Identity, C1, C0)
-    act(V("ra", C, 2 * C), IDENT)
-    act(V("rb", C, 2 * C), IDENT)
-    for n in ("wr0", "wr1", "wr2", "wra", "wrb"):
-        fill(V(n, 0, 16), 0.0)
-        fill(V(n, 336, 352), 0.0)
-    QL, ML, KN, KXO, KXB = [V(n, 0, 20) for n in ("ql", "ml", "kn", "kxo", "kxb")]
-    WM = V("wmask", 0, C)
-    cp(QL, V("gqi", 0, 20))
-    cp(ML, V("gmi", 0, 20))
-    cp(V("ar", 0, C), IDENT, QL)
-    act(V("mr", 0, C), IDENT, AF.Copy, 1.0, None, ML)
-    ts(V("z1", 0, 20), V("gqi", 0, 20), -160.0, None, OP.add)
-    tt(V("wr0", 16, 336), V("ar", 0, C), WM, OP.mult, ML)
-
-    def turn(n):
-        tr(V("ta", 0, C), V(n, 16, 336))
-        tr(V("tb", 0, 352), V(n, 0, 352))
-
-    def entries(out, lo):
-        tt(V(out, lo, lo + 20, 2), V("ta", 1, C, 32), V("tb", 17, C, 32), OP.add)
-        tt(V(out, lo + 1, lo + 20, 2), V("ta", 18, C, 32), V("tb", 34, 352, 32), OP.add)
-
-    def spread(z, zd, rep, w, rdsem):
-        for k in range(8):
-            dma("y", w, T[zd][:, :, 20 * k:20 * k + 20], T[z][16 * k:16 * k + 16, 0:40], [V(z, 0, 40, 1, 16 * k, 16 * k + 16)],
-                [V(zd, 40 * k, 40 * k + 40)])
-        for k in range(8):
-            dma("y", rdsem, T[rep][16 * k:16 * k + 16, 0:320], T[zd][:, :, :], [V(zd, 0, 320)], [V(rep, 0, 320, 1, 16 * k, 16 * k + 16)])
-
-    turn("wr0")
-    entries("z1", 20)
-    spread("z1", "zd1", "rep1", "zw1", "zr1")
+    def unpacker(b):
+        sel(V("et", 512 * b, 512 * b + 512), V("ones", 0, 512), [[1, 128], [1000, 4]], OP.is_equal, -1000 * b, -1)
+    unpacker(0)
+    unpacker(1)
+    for n in ("ar", "br", "tin", "wra"):
+        pads(n)
+    ts(i0, pid, 15, None, OP.bitwise_and)
+    ts(i1, pid, 4, 1, OP.arith_shift_right, OP.bitwise_and)
+    ts(i2, pid, 1, None, OP.bitwise_and)
+    cp(L16, i0)
+    cp(ODD, i1)
+    ts(T1, i2, -672.0, 320.0, OP.mult, OP.add)
+    ts(H1, i2, 336.0, None, OP.mult)
+    ts(W("wi"), W("w16"), L16, None, OP.add)
+    ts(HH, T1, ODD, H1, OP.mult, OP.add)
+    ts(EVEN, i1, -1.0, 1.0, OP.mult, OP.add)
+    J, J16, B1, B2, B3 = V("wi", 0, 4), V("t20", 0, 4), V("t20", 4, 8), V("t20", 8, 12), V("t20", 12, 16)
+    ts(J16, J, 59.0, 16.0, OP.min, OP.mult)
+    ts(B2, J, 40.0, -304.0, OP.is_ge, OP.mult)
+    ts(B1, J, 20.0, -336.0, OP.is_ge, OP.mult)
+    ts(HO, ODD, 16.0, HH, OP.mult, OP.add)
+    tt(J16, J16, B2, OP.add)
+    ts(B3, J, 19.0, 16.0, OP.min, OP.mult)
+    tt(B2, J16, B1, OP.add)
+    ts(V("own", 0, 2), V("t20", 12, 14), HO, None, OP.add)
+    ts(V("clo", 0, 4), B2, HH, 16.0, OP.add, OP.add)
+    ts(W("we"), W("wi"), EVEN, None, OP.mult)
+    ts(V("offo", 20, 180), V("i160", 0, 160), L16, None, OP.add)
+    ts(B1, J, 20.0, -320.0, OP.is_ge, OP.mult)
+    ts(W("wo"), W("wi"), ODD, None, OP.mult)
+    tt(B2, J16, B1, OP.add)
+    pads("mn")
+    pads("wrb")
+    ts(V("offb", 20, 180), V("i160", 0, 160), L16, None, OP.add)
+    ts(V("clb", 0, 4), B2, HH, None, OP.add)
+    cp(W("ql"), W("gqi"))
+    cp(W("ml"), W("gmi"))
+    gather("ar", "ident", "ql")
     ts(V("ints", 16, 24), V("ints", 8, 16), 127, None, OP.bitwise_and)
+    gather("br", "ar", "ml")
     cp(V("ul", 0, 8), V("ints", 16, 24))
-    qz("um", 0, 128, V("ut", 0, 512))
-    op("v", lambda: g.vector.tensor_copy(T.u2q[:, 0:128].bitcast(dt.uint32), T.umq[:, 0:128].bitcast(dt.uint32).indirect(T.ul[:, 0:8])),
-       [V("umq", 0, 128), V("ul", 0, 8)], [V("u2q", 0, 128)])
-    op("s", lambda: g.scalar.activation(T.u2s[:, 0:128], T.ums[:, 0:128].indirect(T.ul[:, 0:8]), AF.Copy),
-       [V("ums", 0, 128), V("ul", 0, 8)], [V("u2s", 0, 128)])
-    qz("xm0", 0, C, V("x0", 0, 4 * C))
-    mm("ps0", C, "u2", 0, "xm0")
-    cp(V("gmf", 0, 20), V("gmi", 0, 20))
-    ts(V("wi", 0, 20), V("w16", 0, 20), L16, None, OP.add)
-    tt(V("kap", 0, 20), V("gmf", 0, 20), V("wi", 0, 20), OP.min)
-    cp(V("kxo", 0, 20, 2), V("kap", 0, 10))
-    cp(V("kxo", 1, 20, 2), V("kap", 10, 20))
-    ts(MT2, MT, 2.0, None, OP.mult)
-    ts(MTN, MT, -1.0, None, OP.mult)
-    act(V("pho", 0, C), V("phi0", 0, C), AF.Copy, MT)
-    act(V("phb", 0, C), V("phi0", 0, C), AF.Copy, MT)
-    ts(L32B, L32, -16.0, None, OP.add)
-    ts(V("ct", 0, 512), V("cpat", 0, 512), L32, None, OP.is_equal)
-    ts(V("ct", 512, 1024), V("cpat", 0, 512), L32B, None, OP.is_equal)
-    qz("cm", 0, 256, V("ct", 0, 1024))
+    act(R("mr"), IDENT, AF.Copy, 1.0, None, W("ml"))
+
+    def table(d, a, keep, idle):
+        tt(V(d, 0, 64), V("zc", 0, 64), V("za", 0, 64), OP.subtract)
+        ts(V(a, 0, 64), V("za", 0, 64), 160.0, None, OP.add)
+        ts(W(d), W(d), keep, None, OP.mult)
+        ts(W(a), W(a), keep, None, OP.mult)
+        tt(W(a), W(a), W(idle), OP.add)
 
     def halves(X):
         for b in range(4):
             act(V("xh", C * b, C * b + C), V(X, b, 4 * C, 4), AF.Copy, 0.5)
-        act(V("xi", 0, 4 * C), V(X, 0, 4 * C), AF.Copy, 0.5)
+            sel(V("xi", C * b, C * b + C), V("xh", C * b, C * b + C), [[0, C]], OP.is_gt, 1, 0)
+
+    def scores(xm, k):
+        mm("ps%d" % (4 + k), "u2", 0, xm, PARTS[k][0], PARTS[k][1])
+
+    turn("ar")
+    tt(W("kap"), W("gmi"), W("wi"), OP.min)
+    cp(V("za", 0, 64), TURNED, V("clo", 0, 4))
+    qz("um", 0, 128, "ut")
+    cp(W("kn"), W("kap"))
+    op("v", lambda: g.vector.tensor_copy(T.u2q[:, 0:128].bitcast(dt.uint32), T.umq[:, 0:128].bitcast(dt.uint32).indirect(T.ul[:, 0:8])),
+       [V("umq", 0, 128), V("ul", 0, 8)], [V("u2q", 0, 128)])
+    op("s", lambda: g.scalar.activation(T.u2s[:, 0:128], T.ums[:, 0:128].indirect(T.ul[:, 0:8]), AF.Copy),
+       [V("ums", 0, 128), V("ul", 0, 8)], [V("u2s", 0, 128)])
+    qz("xm", 0, C, "x0")
+    scores("xm", 0)
+    scores("xm", 1)
     halves("x0")
+    unpacker(2)
+    unpacker(3)
+    turn("br")
+    cp(V("zc", 0, 64), TURNED, V("clo", 0, 4))
+    table("do", "ao", ODD, "we")
 
-    def differ(rep):
-        A, B = V(rep, 0, 160), V(rep, 160, 320)
-        tt(V("dd", 0, 160), B, A, OP.subtract)
-        tt(V("sm", 0, 160), B, A, OP.add)
+    def places(kx, phi, cl, d, a, off, between=None):
+        for k, (lo, hi) in enumerate(PARTS):
+            ts(V("sg", lo, hi), V("ps%d" % (4 + k), 0, hi - lo), 0.0, None, OP.is_gt)
+        if phi:
+            tt(R("tin"), R("sg"), R(phi), OP.is_equal, W(kx))
+        else:
+            cp(R("tin"), R("sg"), W(kx))
+        turn("tin")
+        if between:
+            between()
+        tt(V("ft", 0, 64), TURNED, V(d, 0, 64), OP.mult, V(cl, 0, 4))
+        tt(V("ff", 0, 60), V("ft", 0, 60), V(a, 0, 60), OP.add)
+        cp(V(off, 0, 60), V("ff", 0, 60))
 
-    def tables(H, W):
-        for k in range(8):
-            o = 4 * (k % 2) + k // 2
-            act(V(H, o, 160, 8), V("dd", 20 * k, 20 * k + 20))
-            act(V(W, o, 160, 8), V("sm", 20 * k, 20 * k + 20), AF.Identity, 0.5, V("own", k, k + 1))
+    def hand(off, down):
+        def move(a, n, d):
+            f, t = (a, a + 32 * d) if down else (128 - a - n, 128 - a - n - 32 * d)
+            return lambda: cp(V(off, 20 + 40 * d, 20 + 80 * d, 1, t, t + n), V(off, 20, 20 + 40 * d, 1, f, f + n))
+        return [move(0, 32, 1), move(32, 32, 1), move(64, 32, 1), move(0, 64, 2)]
 
-    def bits(kx, phi):
-        ts(V("sg", 0, C), V("ps0", 0, C), 0.0, 0.5, OP.is_gt, OP.subtract)
-        tt(V("tin", 0, C), V("sg", 0, C), V(phi, 0, C), OP.mult, kx)
-        tr(V("tl", 0, C), V("tin", 0, C))
-        qz("lm", 0, 128, V("tl", 0, 512))
-        mm("ps1", 128, "cm", 0, "lm")
-        mm("ps2", 128, "cm", 128, "lm")
+    def chain(off, order, last, beside, work=None):
+        cur = "ident"
+        for n, o in enumerate(order):
+            nxt = last if last and n == 7 else ("ra", "rb")[n % 2]
+            if work and 2 <= n < 7:
+                act(R(nxt), R(cur), AF.Copy, 1.0, None, V(off, o, o + 20))
+            else:
+                if work and n == 7:
+                    work()
+                gather(nxt, cur, off, o)
+            for f in beside[2 * n:2 * n + 2]:
+                f()
+            cur = nxt
+        return cur
 
-    def places(H, W):
-        for h in range(2):
-            a, b = 80 * h, 80 * h + 80
-            tt(V("ft", a, b), V("ps%d" % (1 + h), 0, 80), V(H, a, b), OP.mult)
-        for h in range(2):
-            a, b = 80 * h, 80 * h + 80
-            tt(V("ff", a, b), V("ft", a, b), V(W, a, b), OP.add)
+    def inverse():
+        op("v", lambda: g.vector.tensor_copy(T.br[:, PAD:PAD + C].indirect(T.ql[:, 0:20]), ap(IDENT)), [IDENT, W("ql")], [R("br")])
+        turn("br")
+        entries("n0l", 160.0)
+        cp(V("za", 0, 64), TURNED, V("clb", 0, 4))
+        cp(R("mn"), R("mr"), W("n0l"))
+        entries("n0w", 160.0)
+        turn("mn")
+        entries("mnw", 160.0)
+        cp(V("zc", 0, 64), TURNED, V("clb", 0, 4))
 
-    def listed(g_):
-        k = 4 * (g_ % 2) + g_ // 2
-        cp(V("off", 20 * g_, 20 * g_ + 20), V("ff", k, 160, 8))
+    def send(rnd):
+        hm, partner = "hm%d" % rnd, T.cores[rank ^ STEP[rnd]]
+        hq, hs = T[hm + "q"], T[hm + "s"]
+        M["deps"]("g", [R(hm + "q"), R(hm + "s")], [])
+        way = _relays(topo, core, partner)
+        if way:
+            fq = []
+            for i in range(2):
+                a, b = C // 2 * i, C // 2 * (i + 1)
+                rid, p = topo.addr(way[i], core)
+                e = topo.engines(core, way[i])
+                m = sum(1 << x for x in e[len(e) // 2 * i:len(e) // 2 * (i + 1)])
+                fq.append(RemoteDMATransfer(dst_ids=[DstId(rid=rid, pnc=p)], dma_engine_mask=m, remote_sem=T.sem.rarr,
+                                            src=hq[:, a:b].bitcast(dt.uint8), dst=T.relq[:, a:b].bitcast(dt.uint8)))
+            g.remote_dma_fused(fq, local_sem=T.sem.sent)
+            rid, p = topo.addr(way[2], core)
+            m = topo.mask(core, way[2])
+            g.remote_dma(T.rels[:, 0:C], hs[:, 0:C], T.sem.rarr, T.sem.sent, p, rid, m)
+        else:
+            rid, p = topo.addr(partner, core)
+            m, arr = topo.mask(core, partner), T.sem["arr%d" % rnd]
+            g.remote_dma(T["land%dq" % rnd][:, 0:C].bitcast(dt.uint8), hq[:, 0:C].bitcast(dt.uint8), arr, T.sem.sent, p, rid, m)
+            g.remote_dma(T["land%ds" % rnd][:, 0:C], hs[:, 0:C], arr, T.sem.sent, p, rid, m)
+        M["cnt"]["sent"] = M["cnt"].get("sent", 0) + 2 * _count(m)
 
-    def step(a, b, g_):
-        o = 20 * g_
-        act(V(b, 160, 320), V(a, 0, 2 * C), AF.Copy, 1.0, None, V("off", o + 10, o + 20))
-        cp(V(b, 0, 160), V(a, 0, 2 * C), V("off", o, o + 10))
-
-    bits(KXO, "pho")
-    for b in range(4):
-        sel(V("et", 512 * b, 512 * b + 512), V("ones", 0, 512), [[1, 128], [1000, 4]], OP.is_equal, -1000 * b, -1)
-    op("v", lambda: g.vector.tensor_copy(T.n0[:, 0:C].indirect(T.ql[:, 0:20]), ap(IDENT)), [IDENT, QL], [V("n0", 0, C)])
-    ts(V("own", 0, 8), V("own", 0, 8), 160.0, None, OP.add)
-    differ("rep1")
-    tables("hso", "mso")
-    tt(V("wr1", 16, 336), V("n0", 0, C), WM, OP.mult)
-    turn("wr1")
-    entries("z2", 0)
-    ts(V("n0l", 0, 20), V("z2", 0, 20), 160.0, None, OP.add)
-    tt(V("wr2", 16, 336), V("mr", 0, C), WM, OP.mult, V("n0l", 0, 20))
-    turn("wr2")
-    entries("z2", 20)
-    spread("z2", "zd2", "rep2", "zw2", "zr2")
+    def layer(k, js):
+        a, b = PARTS[k]
+        for j in js:
+            mm("ps%d" % j, "wm", 128 * j, "vm", a, b)
+            act(V("hh", 4 * a + j, 4 * b, 4), V("ps%d" % j, 0, b - a), AF.Copy, 0.03125)
 
     for rnd in range(3):
-        Y, VV, HH = "x%d" % (1 + rnd % 2), "vv", "hh"
-        vm, hm, land = "vm%d" % rnd, "hm%d" % rnd, "land%d" % rnd
+        Y, hm, land = "x%d" % (1 + rnd % 2), "hm%d" % rnd, "land%d" % rnd
+        phi = (None, "ee0", "cum")[rnd]
         partner = T.cores[rank ^ STEP[rnd]]
         if rnd:
-            bits(KXO, "pho")
-        places("hso", "mso")
-        cur, nxt = "ra", "rb"
-        listed(7)
-        listed(6)
-        for g_ in range(7, 0, -1):
-            step(cur, nxt, g_)
-            if g_ > 1:
-                listed(g_ - 2)
-            cur, nxt = nxt, cur
-        tt(V("wra", 16, 336), V(cur, 0, 2 * C), WM, OP.mult, V("off", 0, 20))
+            halves("x%d" % rnd)
+        places("kn", phi, "clo", "do", "ao", "offo")
+        chain("offo", [0, 20, 80, 60, 120, 100, 160, 140], "wra", hand("offo", True), None if rnd else inverse)
         turn("wra")
-        entries("wf", 0)
-        ts(V("aoff", 0, 20), V("wf", 0, 20), 160.0, None, OP.add)
-        for b in range(4):
-            tt(V(VV, b, 4 * C, 4), V("xh", C * b, C * b + C), V("xi", b, 4 * C, 4), OP.add, V("aoff", 0, 20))
-        for k in range(8):
-            dma("y", "a8s%d" % rnd, T.a8[16 * k:16 * k + 16, 0:20], T.aoff[112:128, 0:20], [V("aoff", 0, 20, 1, 112, 128)],
-                [V("a8", 0, 20, 1, 16 * k, 16 * k + 16)])
-        dma("y", "ashs%d" % rnd, T.ash[16:128, 0:C], T.wra[0:112, 16:336], [V("wra", 16, 336, 1, 0, 112)], [V("ash", 0, C, 1, 16, 128)])
-        qz(vm, 0, C, V(VV, 0, 4 * C))
-        mm("ps0", C, "u2", 0, vm)
+        entries("aoff", 160.0)
+        dma("y", "ashs%d" % rnd, T.ash[16:128, 0:C], T.wra[0:112, PAD:PAD + C], [V("wra", PAD, PAD + C, 1, 0, 112)], [V("ash", 0, C, 1, 16, 128)])
+        for k in (96, 112):
+            dma("y", "a8s%d" % rnd, T.a8[k:k + 16, 0:20], T.aoff[112:128, 0:20], [V("aoff", 0, 20, 1, 112, 128)], [V("a8", 0, 20, 1, k, k + 16)])
         if rnd == 0:
-            differ("rep2")
-            tables("hsb", "msb")
-        for b in range(4):
-            mm("ps%d" % (4 + b), C, "wm", 128 * b, vm)
-            act(V(HH, b, 4 * C, 4), V("ps%d" % (4 + b), 0, C), AF.Copy, 0.03125)
-        if rnd == 0:
-            tt(V("kb", 0, 20), V("z2", 0, 20), V("z2", 20, 40), OP.min)
-            ts(V("kxb", 0, 20, 2), V("kb", 0, 10), 160.0, None, OP.add)
-            ts(V("kxb", 1, 20, 2), V("kb", 10, 20), 160.0, None, OP.add)
-            cp(V("ash", 0, C, 1, 0, 16), V("rb", C, 2 * C, 1, 0, 16))
-        bits(KXB, "phb")
-        if rnd == 0:
-            qz("em", 0, 512, V("et", 0, 2048))
-            qz("vw", 0, 128, V("vt", 0, 512))
-        places("hsb", "msb")
-        cur, nxt = "ra", "rb"
-        listed(0)
-        listed(1)
-        for g_ in range(8):
-            step(cur, nxt, g_)
-            if g_ == 0:
-                qz(hm, 0, C, V(HH, 0, 4 * C))
-            if g_ < 6:
-                listed(g_ + 2)
-            if g_ == 0:
-                M["deps"]("g", [V(hm + "q", 0, C), V(hm + "s", 0, C)], [])
-                hq, hs, lq, ls = T[hm + "q"], T[hm + "s"], T[land + "q"], T[land + "s"]
-                way = _relays(topo, core, partner)
-                tot = 0
-                if not way:
-                    rid, p = topo.addr(partner, core)
-                    m = topo.mask(core, partner)
-                    g.remote_dma(lq[:, 0:C].bitcast(dt.uint8), hq[:, 0:C].bitcast(dt.uint8), T.sem["arr%d" % rnd], T.sem.sent, p, rid, m)
-                    g.remote_dma(ls[:, 0:C], hs[:, 0:C], T.sem["arr%d" % rnd], T.sem.sent, p, rid, m)
-                    tot, got = 2 * _count(m), 2 * _count(m)
-                else:
-                    got, fq, fs = 0, [], []
-                    for i, k in enumerate(way):
-                        a, b = 160 * i, 160 * i + 160
-                        rid, p = topo.addr(k, core)
-                        e = topo.engines(core, k)
-                        n = len(e) // len(way)
-                        m = sum(1 << x for x in e[n * i:n * i + n])
-                        to = [DstId(rid=rid, pnc=p)]
-                        fq.append(RemoteDMATransfer(dst_ids=to, dma_engine_mask=m, remote_sem=T.sem.rarrq,
-                                                    src=hq[:, a:b].bitcast(dt.uint8), dst=T.relq[:, 0:160].bitcast(dt.uint8)))
-                        fs.append(RemoteDMATransfer(dst_ids=to, dma_engine_mask=m, remote_sem=T.sem.rarrs,
-                                                    src=hs[:, a:b], dst=T.rels[:, 0:160]))
-                        tot += 2 * n
-                    g.remote_dma_fused(fq, local_sem=T.sem.sent)
-                    g.remote_dma_fused(fs, local_sem=T.sem.sent)
-                    for k in _relays(topo, partner, core):
-                        got += 2 * _count(topo.mask(k, core))
-                M["cnt"]["sent"] = M["cnt"].get("sent", 0) + tot
-            cur, nxt = nxt, cur
-        tt(V("wrb", 16, 336), V(cur, 0, C), WM, OP.mult, V("a8", 0, 20))
-        turn("wrb")
-        entries("wf", 0)
-        ts(V("boff", 0, 20), V("wf", 0, 20), 160.0, None, OP.add)
-        M["arrived"]("t", "arr%d" % rnd, got, [])
-        for b in range(4):
-            mm("ps%d" % (4 + b), C, "em", 128 * b, land)
-            act(V("dsb", C * b, C * b + C), V("ps%d" % (4 + b), 0, C))
-        ph, pn = ("phi0", "phi1") if rnd % 2 == 0 else ("phi1", "phi0")
-        tt(V("ee", 0, C), V("wrb", 16, 336), V("ash", 0, C), OP.is_equal)
-
-        def new(b):
-            tt(V(Y, b, 4 * C, 4), V("dsb", C * b, C * b + C), V(VV, b, 4 * C, 4), OP.add, V("boff", 0, 20))
-        new(0)
-        tt(V(pn, 0, C), V(ph, 0, C), V("ee", 0, C), OP.is_equal)
-        new(1)
-        if rnd < 2:
-            act(V("pho", 0, C), V(pn, 0, C), AF.Identity, MT2, MTN, KXO)
-            act(V("phb", 0, C), V(pn, 0, C), AF.Identity, MT2, MTN, KXB)
-        new(2)
-        new(3)
-        qz("xm%d" % (rnd + 1), 0, C, V(Y, 0, 4 * C))
-        if rnd < 2:
-            mm("ps0", C, "u2", 0, "xm%d" % (rnd + 1))
-            halves(Y)
+            act(V("ash", 0, C, 1, 0, 16), V("ident", 0, C, 1, 0, 16))
         else:
-            mm("ps0", C, "vw", 0, "xm3")
-            dma("y", "oend", T.oc[:, 0:4 * C], T.xm3q[:, 0:C].bitcast(dt.uint8), [V("xm3q", 0, C)], [])
-            act(V("yt", 0, C), V("ps0", 0, C))
-            dma("s", "oend", T.y[:], T.yt[:], [V("yt", 0, C)], [])
-            for k in range(4):
-                dma("y", "oend", T.osc[4 * k:4 * k + 4, 0:C], T.xm3s[32 * k:32 * k + 4, 0:C], [V("xm3s", 0, C)], [])
-            cp(KN, V("kap", 0, 20))
-            tt(V("amb", 0, C), V("ar", 0, C), V("wr0", 16, 336), OP.subtract)
-            tt(V("t1", 0, C), V(pn, 0, C), V("amb", 0, C), OP.mult, KN)
-            ts(V("b160", 0, C), V("wr0", 16, 336), 160.0, None, OP.add)
-            tt(V("qf", 0, C), V("t1", 0, C), V("b160", 0, C), OP.add)
-            dma("y", "oend", T.qo[:], T.qf[0:128:16, 0:C], [V("qf", 0, C)], [])
+            act(R("phb"), R(phi), AF.Copy, 1.0, None, W("n0l"))
+        for k, (a, b) in enumerate(PARTS):
+            for j in range(4):
+                tt(V("vv", 4 * a + j, 4 * b, 4), V("xh", C * j, C * j + C), V("xi", C * j + a, C * j + b), OP.add, V("aoff", a // 16, b // 16))
+            qz("vm", a, b, "vv")
+            scores("vm", k)
+            if k == 0:
+                layer(0, range(3))
+        layer(0, [3])
+        layer(1, range(4))
+        if rnd == 0:
+            tt(W("kap"), W("n0w"), W("mnw"), OP.min)
+            table("db", "ab", EVEN, "wo")
+            cp(W("kxb"), W("kap"))
+        places("kxb", phi and "phb", "clb", "db", "ab", "offb", lambda: qz(hm, 0, C, "hh"))
+        send(rnd)
+        act(R("ak"), R("ash"), AF.Copy, 1.0, None, W("kn"))
+        spread = [lambda q=q: cp(V("a8", 0, 20, 1, 32 * q, 32 * q + 32), V("a8", 0, 20, 1, 96, 128)) for q in range(3)]
+        extra = [[lambda: qz("em", 0, 256, "et"), lambda: pads("cum"), lambda: qz("em", 256, 512, "et")],
+                 [lambda: qz("vw", 0, 128, "vt"), lambda: pads("ee2"), lambda: fill(C160, 160.0), lambda: tt(W("dm"), W("gmi"), W("wi"), OP.subtract)],
+                 []][rnd]
+        cur = chain("offb", [0, 40, 60, 80, 100, 120, 140, 160], None, hand("offb", False) + extra + spread)
+        gather("wrb", cur, "a8")
+        turn("wrb")
+        entries("boff", 160.0)
+        way = _relays(topo, partner, core) or [partner, partner]
+        M["arrived"]("t", "arr%d" % rnd, sum(_count(topo.mask(k, core)) for k in way))
+        for j in range(4):
+            mm("ps%d" % j, "em", 128 * j, land, 0, C)
+            act(V("dsb", C * j, C * j + C), V("ps%d" % j, 0, C))
+        ee = "ee%d" % rnd
+        tt(R(ee), R("wrb"), R("ak"), OP.is_equal, W("kn"))
+        if rnd == 1:
+            tt(R("cum"), R("ee0"), R("ee1"), OP.is_equal)
+            turn("cum")
+            entries("c1w", 0.0)
+        for j in range(3):
+            tt(V(Y, j, 4 * C, 4), V("dsb", C * j, C * j + C), V("vv", j, 4 * C, 4), OP.add, W("boff"))
+        for k, (a, b) in enumerate(PARTS):
+            tt(V(Y, 4 * a + 3, 4 * b, 4), V("dsb", 3 * C, 4 * C), V("vv", 4 * a + 3, 4 * b, 4), OP.add, V("boff", a // 16, b // 16))
+            qz("xm", a, b, Y)
+            if rnd < 2:
+                scores("xm", k)
+            else:
+                mm("ps%d" % (4 + k), "vw", 0, "xm", a, b)
+                act(V("yt", a, b), V("ps%d" % (4 + k), 0, b - a))
+    dma("y", "oend", T.oc[:, 0:4 * C], T.xmq[:, 0:C].bitcast(dt.uint8), [R("xmq")], [])
+    dma("s", "oend", T.y[:], T.yt[:], [R("yt")], [])
+    for k in range(4):
+        dma("y", "oend", T.osc[4 * k:4 * k + 4, 0:C], T.xms[32 * k:32 * k + 4, 0:C], [R("xms")], [])
+    turn("ee2")
+    entries("e2w", 0.0)
+    tt(W("fw"), W("e2w"), W("c1w"), OP.not_equal)
+    tt(W("fw"), W("fw"), W("dm"), OP.mult)
+    tt(W("fw"), W("fw"), W("wi"), OP.add)
+    cp(W("qoff"), W("fw"))
+    ts(R("qf"), R("ar"), 160.0, None, OP.add, None, W("qoff"))
+    dma("y", "oend", T.qo[:], T.qf[0:128:16, 0:C], [R("qf")], [])
     M["finish"]()

@@ -4,12 +4,13 @@ from concourse.mybir import dt, AluOpType, ActivationFunctionType
 C, N = 320, 8
 STEP = [4, 1, 2]
 PARTS = [(0, 192), (192, 320)]
+SENDS = [[(0, C)]] * 3
 PAD = 16
 PADDED = ("ar", "br", "mn", "tin", "wra", "wrb", "ee2", "cum")
 OP, AF = AluOpType, ActivationFunctionType
 
 SCRATCH = {}
-SEMAPHORES = ["cv", "cs", "ct", "cg", "sent", "rarr", "rsent", "dq", "dm", "dx", "du", "dw", "dv", "oend"]
+SEMAPHORES = ["cv", "cs", "ct", "cg", "sent", "rarr0", "rsent", "dq", "dm", "dx", "du", "dw", "dv", "oend"]
 
 
 def _declare():
@@ -26,7 +27,6 @@ def _declare():
         mx("land%d" % r, C)
         SEMAPHORES.extend(["arr%d" % r, "a8s%d" % r, "ashs%d" % r])
     mx("rel", C)
-    mx("um", 128)
     mx("u2", 128)
     mx("vw", 128)
     mx("wm", 512)
@@ -46,15 +46,14 @@ def _declare():
     sb("i160", 160, "float32")
     for n in ("za", "zc", "do", "ao", "db", "ab", "ft", "ff"):
         sb(n, 64, "float32")
-    for n in ("w16", "wi", "we", "wo", "kap", "dm", "fw", "t20"):
+    for n in ("w16", "wi", "we", "wo", "kap", "fw", "t20"):
         sb(n, 20, "float32")
-    for n in ("c1w", "e2w", "n0w", "mnw"):
+    for n in ("c1w", "e2w", "n0w", "mnw", "dm"):
         sb(n, 32, "float32")
     sb("cols", 16, "float32")
     for n in ("gqi", "gmi"):
         sb(n, 20, "int32")
-    sb("ints", 24, "int32")
-    sb("ul", 8, "uint16")
+    sb("ints", 4, "int32")
     for n in ("ql", "ml", "kn", "kxb", "a8", "qoff"):
         sb(n, 20, "uint16")
     for n in ("aoff", "boff", "n0l"):
@@ -194,14 +193,15 @@ def _relay_program(g, core, T, topo):
             rid, pid = topo.addr(dst, core)
             m, e = topo.mask(core, dst), _count(topo.mask(src, core))
             lq, ls, arr = T["land%dq" % s], T["land%ds" % s], T.sem["arr%d" % s]
-            if i < 2:
-                a, b = C // 2 * i, C // 2 * (i + 1)
-                g.wait_ge(T.sem.rarr, e // 2)
-                g.remote_dma(lq[:, a:b].bitcast(dt.uint8), T.relq[:, a:b].bitcast(dt.uint8), arr, T.sem.rsent, pid, rid, m)
-            else:
-                g.wait_ge(T.sem.rarr, e)
-                g.remote_dma(ls[:, 0:C], T.rels[:, 0:C], arr, T.sem.rsent, pid, rid, m)
-            g.wait_ge(T.sem.rsent, _count(m))
+            for k, (lo, hi) in enumerate(SENDS[s]):
+                if i < 2:
+                    a, b = lo + (hi - lo) // 2 * i, lo + (hi - lo) // 2 * (i + 1)
+                    g.wait_ge(T.sem["rarr%d" % k], e // 2)
+                    g.remote_dma(lq[:, a:b].bitcast(dt.uint8), T.relq[:, a:b].bitcast(dt.uint8), arr, T.sem.rsent, pid, rid, m)
+                else:
+                    g.wait_ge(T.sem["rarr%d" % k], e)
+                    g.remote_dma(ls[:, lo:hi], T.rels[:, lo:hi], arr, T.sem.rsent, pid, rid, m)
+            g.wait_ge(T.sem.rsent, len(SENDS[s]) * _count(m))
 
 
 def rank_program(g, core, T, topo):
@@ -290,17 +290,16 @@ def rank_program(g, core, T, topo):
     dma("y", "dq", T.gqi[:], T.gq[:], [], [W("gqi")])
     dma("s", "dm", T.gmi[:], T.gm[:], [], [W("gmi")])
     dma("y", "dx", T.x0[:], T.x[:], [], [V("x0", 0, 4 * C)])
-    dma("s", "du", T.ut[:], T.u[:], [], [V("ut", 0, 512)])
-    dma("y", "dw", T.wmq[:, 0:512].bitcast(dt.uint8), T.wc[:, 0:2048], [], [V("wmq", 0, 512)])
+    dma("s", "du", T.ut[:, 64:512], T.u[:, 0:448], [], [V("ut", 64, 512)])
+    dma("s", "du", T.ut[:, 0:64], T.u[:, 448:512], [], [V("ut", 0, 64)])
+    dma("y", "dw", T.wmq[:, 0:512].bitcast(dt.uint8), T.wc[:, 0:2048], [V("x0", 0, 4 * C)], [V("wmq", 0, 512)])
     dma("y", "dw", T.wms[:, 0:512], T.ws[:, 0:512], [], [V("wms", 0, 512)])
-    dma("y", "dv", T.vt[:], T.v[:], [], [V("vt", 0, 512)])
     IDENT = R("ident")
     pid, i0, i1, i2 = [V("ints", k, k + 1) for k in range(4)]
     iota(pid, [[1, 1]], 0, 1, False)
     iota(W("w16"), [[16, 20]], 0, 0)
     iota(IDENT, [[1, C]], -160, 0)
     iota(V("i160", 0, 160), [[0, 8], [16, 20]], 0, 0)
-    iota(V("ints", 8, 16), [[16, 8]], 112, 0, False)
     iota(V("ones", 0, 512), [[0, 512]], 1, 0)
 
     def unpacker(b):
@@ -331,27 +330,20 @@ def rank_program(g, core, T, topo):
     ts(V("clo", 0, 4), B2, HH, 16.0, OP.add, OP.add)
     ts(W("we"), W("wi"), EVEN, None, OP.mult)
     ts(V("offo", 20, 180), V("i160", 0, 160), L16, None, OP.add)
-    ts(B1, J, 20.0, -320.0, OP.is_ge, OP.mult)
-    ts(W("wo"), W("wi"), ODD, None, OP.mult)
-    tt(B2, J16, B1, OP.add)
-    pads("mn")
-    pads("wrb")
-    ts(V("offb", 20, 180), V("i160", 0, 160), L16, None, OP.add)
-    ts(V("clb", 0, 4), B2, HH, None, OP.add)
     cp(W("ql"), W("gqi"))
     cp(W("ml"), W("gmi"))
     gather("ar", "ident", "ql")
-    ts(V("ints", 16, 24), V("ints", 8, 16), 127, None, OP.bitwise_and)
-    gather("br", "ar", "ml")
-    cp(V("ul", 0, 8), V("ints", 16, 24))
+    tt(W("kap"), W("gmi"), W("wi"), OP.min)
+    act(R("br"), R("ar"), AF.Copy, 1.0, None, W("ml"))
+    cp(W("kn"), W("kap"))
     act(R("mr"), IDENT, AF.Copy, 1.0, None, W("ml"))
 
     def table(d, a, keep, idle):
+        ts(W("fw"), W("za"), 160.0, keep, OP.add, OP.mult)
         tt(V(d, 0, 64), V("zc", 0, 64), V("za", 0, 64), OP.subtract)
-        ts(V(a, 0, 64), V("za", 0, 64), 160.0, None, OP.add)
+        ts(V(a, 20, 64), V("za", 20, 64), 160.0, None, OP.add)
+        tt(W(a), W("fw"), W(idle), OP.add)
         ts(W(d), W(d), keep, None, OP.mult)
-        ts(W(a), W(a), keep, None, OP.mult)
-        tt(W(a), W(a), W(idle), OP.add)
 
     def halves(X):
         for b in range(4):
@@ -362,34 +354,39 @@ def rank_program(g, core, T, topo):
         mm("ps%d" % (4 + k), "u2", 0, xm, PARTS[k][0], PARTS[k][1])
 
     turn("ar")
-    tt(W("kap"), W("gmi"), W("wi"), OP.min)
+    ts(B1, J, 20.0, -320.0, OP.is_ge, OP.mult)
     cp(V("za", 0, 64), TURNED, V("clo", 0, 4))
-    qz("um", 0, 128, "ut")
-    cp(W("kn"), W("kap"))
-    op("v", lambda: g.vector.tensor_copy(T.u2q[:, 0:128].bitcast(dt.uint32), T.umq[:, 0:128].bitcast(dt.uint32).indirect(T.ul[:, 0:8])),
-       [V("umq", 0, 128), V("ul", 0, 8)], [V("u2q", 0, 128)])
-    op("s", lambda: g.scalar.activation(T.u2s[:, 0:128], T.ums[:, 0:128].indirect(T.ul[:, 0:8]), AF.Copy),
-       [V("ums", 0, 128), V("ul", 0, 8)], [V("u2s", 0, 128)])
+    ts(W("wo"), W("wi"), ODD, None, OP.mult)
+    tt(B2, J16, B1, OP.add)
+    pads("mn")
+    turn("br")
+    ts(V("clb", 0, 4), B2, HH, None, OP.add)
+    cp(V("zc", 0, 64), TURNED, V("clo", 0, 4))
+    qz("u2", 0, 128, "ut")
     qz("xm", 0, C, "x0")
     scores("xm", 0)
     scores("xm", 1)
     halves("x0")
     unpacker(2)
     unpacker(3)
-    turn("br")
-    cp(V("zc", 0, 64), TURNED, V("clo", 0, 4))
     table("do", "ao", ODD, "we")
 
-    def places(kx, phi, cl, d, a, off, between=None):
+    def places(kx, phi, cl, d, a, off, shared):
         for k, (lo, hi) in enumerate(PARTS):
             ts(V("sg", lo, hi), V("ps%d" % (4 + k), 0, hi - lo), 0.0, None, OP.is_gt)
-        if phi:
-            tt(R("tin"), R("sg"), R(phi), OP.is_equal, W(kx))
+        if shared:
+            gather("tin", "sg", kx)
+            turn("tin")
         else:
-            cp(R("tin"), R("sg"), W(kx))
-        turn("tin")
-        if between:
-            between()
+            for h in range(2):
+                o, l = V("tin", PAD + 160 * h, PAD + 160 * h + 160), V(kx, 10 * h, 10 * h + 10)
+                if phi:
+                    tt(o, R("sg"), V(phi, R(phi)[1] + 160 * h, R(phi)[1] + 160 * h + 160), OP.is_equal, l)
+                else:
+                    cp(o, R("sg"), l)
+            for lo, hi in ((0, 160), (160, C)):
+                tr(V("turned", lo, hi), V("tin", PAD + lo, PAD + hi))
+                tr(V("turned", C + lo, C + hi + 2 * PAD * (lo > 0)), V("tin", lo, hi + 2 * PAD * (lo > 0)))
         tt(V("ft", 0, 64), TURNED, V(d, 0, 64), OP.mult, V(cl, 0, 4))
         tt(V("ff", 0, 60), V("ft", 0, 60), V(a, 0, 60), OP.add)
         cp(V(off, 0, 60), V("ff", 0, 60))
@@ -400,23 +397,22 @@ def rank_program(g, core, T, topo):
             return lambda: cp(V(off, 20 + 40 * d, 20 + 80 * d, 1, t, t + n), V(off, 20, 20 + 40 * d, 1, f, f + n))
         return [move(0, 32, 1), move(32, 32, 1), move(64, 32, 1), move(0, 64, 2)]
 
-    def chain(off, order, last, beside, work=None):
+    def chain(off, order, last, beside, solo):
         cur = "ident"
         for n, o in enumerate(order):
             nxt = last if last and n == 7 else ("ra", "rb")[n % 2]
-            if work and 2 <= n < 7:
+            if n in solo:
                 act(R(nxt), R(cur), AF.Copy, 1.0, None, V(off, o, o + 20))
             else:
-                if work and n == 7:
-                    work()
                 gather(nxt, cur, off, o)
-            for f in beside[2 * n:2 * n + 2]:
+            for f in (beside + [[]] * 8)[n]:
                 f()
             cur = nxt
         return cur
 
     def inverse():
         op("v", lambda: g.vector.tensor_copy(T.br[:, PAD:PAD + C].indirect(T.ql[:, 0:20]), ap(IDENT)), [IDENT, W("ql")], [R("br")])
+        ts(V("offb", 20, 180), V("i160", 0, 160), L16, None, OP.add)
         turn("br")
         entries("n0l", 160.0)
         cp(V("za", 0, 64), TURNED, V("clb", 0, 4))
@@ -425,37 +421,42 @@ def rank_program(g, core, T, topo):
         turn("mn")
         entries("mnw", 160.0)
         cp(V("zc", 0, 64), TURNED, V("clb", 0, 4))
+        pads("wrb")
 
-    def send(rnd):
+    def send(rnd, k):
         hm, partner = "hm%d" % rnd, T.cores[rank ^ STEP[rnd]]
         hq, hs = T[hm + "q"], T[hm + "s"]
-        M["deps"]("g", [R(hm + "q"), R(hm + "s")], [])
+        lo, hi = SENDS[rnd][k]
+        qz(hm, lo, hi, "hh")
+        M["deps"]("g", [V(hm + "q", lo, hi), V(hm + "s", lo, hi)], [])
         way = _relays(topo, core, partner)
         if way:
-            fq = []
+            fq, arr = [], T.sem["rarr%d" % k]
             for i in range(2):
-                a, b = C // 2 * i, C // 2 * (i + 1)
+                a, b = lo + (hi - lo) // 2 * i, lo + (hi - lo) // 2 * (i + 1)
                 rid, p = topo.addr(way[i], core)
                 e = topo.engines(core, way[i])
                 m = sum(1 << x for x in e[len(e) // 2 * i:len(e) // 2 * (i + 1)])
-                fq.append(RemoteDMATransfer(dst_ids=[DstId(rid=rid, pnc=p)], dma_engine_mask=m, remote_sem=T.sem.rarr,
+                fq.append(RemoteDMATransfer(dst_ids=[DstId(rid=rid, pnc=p)], dma_engine_mask=m, remote_sem=arr,
                                             src=hq[:, a:b].bitcast(dt.uint8), dst=T.relq[:, a:b].bitcast(dt.uint8)))
             g.remote_dma_fused(fq, local_sem=T.sem.sent)
             rid, p = topo.addr(way[2], core)
             m = topo.mask(core, way[2])
-            g.remote_dma(T.rels[:, 0:C], hs[:, 0:C], T.sem.rarr, T.sem.sent, p, rid, m)
+            g.remote_dma(T.rels[:, lo:hi], hs[:, lo:hi], arr, T.sem.sent, p, rid, m)
         else:
             rid, p = topo.addr(partner, core)
             m, arr = topo.mask(core, partner), T.sem["arr%d" % rnd]
-            g.remote_dma(T["land%dq" % rnd][:, 0:C].bitcast(dt.uint8), hq[:, 0:C].bitcast(dt.uint8), arr, T.sem.sent, p, rid, m)
-            g.remote_dma(T["land%ds" % rnd][:, 0:C], hs[:, 0:C], arr, T.sem.sent, p, rid, m)
+            g.remote_dma(T["land%dq" % rnd][:, lo:hi].bitcast(dt.uint8), hq[:, lo:hi].bitcast(dt.uint8), arr, T.sem.sent, p, rid, m)
+            g.remote_dma(T["land%ds" % rnd][:, lo:hi], hs[:, lo:hi], arr, T.sem.sent, p, rid, m)
         M["cnt"]["sent"] = M["cnt"].get("sent", 0) + 2 * _count(m)
 
-    def layer(k, js):
-        a, b = PARTS[k]
-        for j in js:
-            mm("ps%d" % j, "wm", 128 * j, "vm", a, b)
-            act(V("hh", 4 * a + j, 4 * b, 4), V("ps%d" % j, 0, b - a), AF.Copy, 0.03125)
+    def same(rnd, h):
+        lo = R("ee%d" % rnd)[1] + 160 * h
+        tt(V("ee%d" % rnd, lo, lo + 160), R("wrb"), V("ak", 160 * h, 160 * h + 160), OP.is_equal, V("kn", 10 * h, 10 * h + 10))
+
+    def summed(out, win, other, off):
+        for j, a, b in [(0, 0, C), (1, 0, C), (2, 0, C)] + [(3, a, b) for a, b in PARTS]:
+            tt(V(out, 4 * a + j, 4 * b, 4), V(win, C * j, C * j + C), other(j, a, b), OP.add, V(off, a // 16, b // 16))
 
     for rnd in range(3):
         Y, hm, land = "x%d" % (1 + rnd % 2), "hm%d" % rnd, "land%d" % rnd
@@ -463,8 +464,10 @@ def rank_program(g, core, T, topo):
         partner = T.cores[rank ^ STEP[rnd]]
         if rnd:
             halves("x%d" % rnd)
-        places("kn", phi, "clo", "do", "ao", "offo")
-        chain("offo", [0, 20, 80, 60, 120, 100, 160, 140], "wra", hand("offo", True), None if rnd else inverse)
+        places("kn", phi, "clo", "do", "ao", "offo", rnd == 0)
+        moves = hand("offo", True)
+        chain("offo", [0, 20, 80, 60, 120, 100, 160, 140], "wra", [moves[:2], moves[2:], [], [], [], [], [] if rnd else [inverse]],
+              [] if rnd else range(2, 7))
         turn("wra")
         entries("aoff", 160.0)
         dma("y", "ashs%d" % rnd, T.ash[16:128, 0:C], T.wra[0:112, PAD:PAD + C], [V("wra", PAD, PAD + C, 1, 0, 112)], [V("ash", 0, C, 1, 16, 128)])
@@ -474,45 +477,47 @@ def rank_program(g, core, T, topo):
             act(V("ash", 0, C, 1, 0, 16), V("ident", 0, C, 1, 0, 16))
         else:
             act(R("phb"), R(phi), AF.Copy, 1.0, None, W("n0l"))
+        summed("vv", "xh", lambda j, a, b: V("xi", C * j + a, C * j + b), "aoff")
         for k, (a, b) in enumerate(PARTS):
-            for j in range(4):
-                tt(V("vv", 4 * a + j, 4 * b, 4), V("xh", C * j, C * j + C), V("xi", C * j + a, C * j + b), OP.add, V("aoff", a // 16, b // 16))
             qz("vm", a, b, "vv")
             scores("vm", k)
-            if k == 0:
-                layer(0, range(3))
-        layer(0, [3])
-        layer(1, range(4))
+        act(R("ak"), R("ash"), AF.Copy, 1.0, None, W("kn"))
+        for j in range(4):
+            mm("ps%d" % j, "wm", 128 * j, "vm", 0, C)
+            act(V("hh", j, 4 * C, 4), V("ps%d" % j, 0, C), AF.Copy, 0.03125)
         if rnd == 0:
             tt(W("kap"), W("n0w"), W("mnw"), OP.min)
             table("db", "ab", EVEN, "wo")
             cp(W("kxb"), W("kap"))
-        places("kxb", phi and "phb", "clb", "db", "ab", "offb", lambda: qz(hm, 0, C, "hh"))
-        send(rnd)
-        act(R("ak"), R("ash"), AF.Copy, 1.0, None, W("kn"))
+        places("kxb", phi and "phb", "clb", "db", "ab", "offb", False)
+        if rnd == 0:
+            dma("y", "dv", T.vt[:], T.v[:], [], [V("vt", 0, 512)])
         spread = [lambda q=q: cp(V("a8", 0, 20, 1, 32 * q, 32 * q + 32), V("a8", 0, 20, 1, 96, 128)) for q in range(3)]
-        extra = [[lambda: qz("em", 0, 256, "et"), lambda: pads("cum"), lambda: qz("em", 256, 512, "et")],
-                 [lambda: qz("vw", 0, 128, "vt"), lambda: pads("ee2"), lambda: fill(C160, 160.0), lambda: tt(W("dm"), W("gmi"), W("wi"), OP.subtract)],
-                 []][rnd]
-        cur = chain("offb", [0, 40, 60, 80, 100, 120, 140, 160], None, hand("offb", False) + extra + spread)
+        extra = [[[lambda b=b: qz("em", 128 * b, 128 * b + 128, "et")] for b in range(4)] + [spread[:2], spread[2:] + [lambda: pads("cum")]],
+                 [[lambda: qz("vw", 0, 128, "vt")], [lambda: pads("ee2")], spread[:2], spread[2:],
+                  [lambda: fill(V("dm", 20, 32), 0.0), lambda: tt(W("dm"), W("gmi"), W("wi"), OP.subtract)]],
+                 [spread[:2], spread[2:]]][rnd]
+        moves = hand("offb", False)
+        cur = chain("offb", [0, 40, 60, 80, 100, 120, 140, 160], None, [moves[:2] + [lambda: send(rnd, 0)], moves[2:]] + extra, [0])
         gather("wrb", cur, "a8")
         turn("wrb")
+        same(rnd, 0)
         entries("boff", 160.0)
+        same(rnd, 1)
         way = _relays(topo, partner, core) or [partner, partner]
-        M["arrived"]("t", "arr%d" % rnd, sum(_count(topo.mask(k, core)) for k in way))
+        M["arrived"]("t", "arr%d" % rnd, len(SENDS[rnd]) * sum(_count(topo.mask(k, core)) for k in way))
         for j in range(4):
             mm("ps%d" % j, "em", 128 * j, land, 0, C)
             act(V("dsb", C * j, C * j + C), V("ps%d" % j, 0, C))
-        ee = "ee%d" % rnd
-        tt(R(ee), R("wrb"), R("ak"), OP.is_equal, W("kn"))
         if rnd == 1:
             tt(R("cum"), R("ee0"), R("ee1"), OP.is_equal)
             turn("cum")
-            entries("c1w", 0.0)
-        for j in range(3):
-            tt(V(Y, j, 4 * C, 4), V("dsb", C * j, C * j + C), V("vv", j, 4 * C, 4), OP.add, W("boff"))
+            tt(V("c1w", 0, 32), TURNED, V("dm", 0, 32), OP.mult, V("own", 0, 2))
+            tt(W("fw"), W("c1w"), W("wi"), OP.add)
+            ts(V("c1w", 0, 32), V("c1w", 0, 32), -2.0, None, OP.mult)
+            tt(V("dm", 0, 32), V("dm", 0, 32), V("c1w", 0, 32), OP.add)
+        summed(Y, "dsb", lambda j, a, b: V("vv", 4 * a + j, 4 * b, 4), "boff")
         for k, (a, b) in enumerate(PARTS):
-            tt(V(Y, 4 * a + 3, 4 * b, 4), V("dsb", 3 * C, 4 * C), V("vv", 4 * a + 3, 4 * b, 4), OP.add, V("boff", a // 16, b // 16))
             qz("xm", a, b, Y)
             if rnd < 2:
                 scores("xm", k)
@@ -524,10 +529,8 @@ def rank_program(g, core, T, topo):
     for k in range(4):
         dma("y", "oend", T.osc[4 * k:4 * k + 4, 0:C], T.xms[32 * k:32 * k + 4, 0:C], [R("xms")], [])
     turn("ee2")
-    entries("e2w", 0.0)
-    tt(W("fw"), W("e2w"), W("c1w"), OP.not_equal)
-    tt(W("fw"), W("fw"), W("dm"), OP.mult)
-    tt(W("fw"), W("fw"), W("wi"), OP.add)
+    tt(V("e2w", 0, 32), TURNED, V("dm", 0, 32), OP.mult, V("own", 0, 2))
+    tt(W("fw"), W("fw"), W("e2w"), OP.add)
     cp(W("qoff"), W("fw"))
     ts(R("qf"), R("ar"), 160.0, None, OP.add, None, W("qoff"))
     dma("y", "oend", T.qo[:], T.qf[0:128:16, 0:C], [R("qf")], [])

@@ -6,7 +6,7 @@ STEP = [4, 1, 2]
 PARTS = [(0, 192), (192, 320)]
 SENDS = [[(0, C)]] * 3
 PAD = 16
-PADDED = ("ar", "br", "mn", "tin", "wra", "wrb", "ee2", "cum")
+PADDED = ("ar", "br", "mn", "tin", "wra", "wrb", "ee2", "cum", "two")
 OP, AF = AluOpType, ActivationFunctionType
 
 SCRATCH = {}
@@ -56,7 +56,7 @@ def _declare():
     sb("ints", 4, "int32")
     for n in ("ql", "ml", "kn", "kxb", "a8", "qoff"):
         sb(n, 20, "uint16")
-    for n in ("aoff", "boff", "n0l"):
+    for n in ("aoff", "boff", "n0l", "pc"):
         sb(n, 32, "uint16")
     for n in ("clo", "clb", "own"):
         sb(n, 4, "uint16")
@@ -358,24 +358,23 @@ def rank_program(g, core, T, topo):
     cp(V("za", 0, 64), TURNED, V("clo", 0, 4))
     ts(W("wo"), W("wi"), ODD, None, OP.mult)
     tt(B2, J16, B1, OP.add)
-    pads("mn")
-    turn("br")
-    ts(V("clb", 0, 4), B2, HH, None, OP.add)
-    cp(V("zc", 0, 64), TURNED, V("clo", 0, 4))
     qz("u2", 0, 128, "ut")
-    qz("xm", 0, C, "x0")
-    scores("xm", 0)
-    scores("xm", 1)
+    for k, (a, b) in enumerate(PARTS):
+        qz("xm", a, b, "x0")
+        scores("xm", k)
     halves("x0")
     unpacker(2)
     unpacker(3)
-    table("do", "ao", ODD, "we")
+    turn("br")
+    ts(V("clb", 0, 4), B2, HH, None, OP.add)
 
     def places(kx, phi, cl, d, a, off, shared):
         for k, (lo, hi) in enumerate(PARTS):
             ts(V("sg", lo, hi), V("ps%d" % (4 + k), 0, hi - lo), 0.0, None, OP.is_gt)
         if shared:
+            cp(V("zc", 0, 64), TURNED, V(cl, 0, 4))
             gather("tin", "sg", kx)
+            table(d, a, ODD, "we")
             turn("tin")
         else:
             for h in range(2):
@@ -387,9 +386,12 @@ def rank_program(g, core, T, topo):
             for lo, hi in ((0, 160), (160, C)):
                 tr(V("turned", lo, hi), V("tin", PAD + lo, PAD + hi))
                 tr(V("turned", C + lo, C + hi + 2 * PAD * (lo > 0)), V("tin", lo, hi + 2 * PAD * (lo > 0)))
-        tt(V("ft", 0, 64), TURNED, V(d, 0, 64), OP.mult, V(cl, 0, 4))
-        tt(V("ff", 0, 60), V("ft", 0, 60), V(a, 0, 60), OP.add)
-        cp(V(off, 0, 60), V("ff", 0, 60))
+        for h in range(2):
+            tt(V("ft", 32 * h, 32 * h + 32), TURNED, V(d, 32 * h, 32 * h + 32), OP.mult, V(cl, 2 * h, 2 * h + 2))
+        for lo, hi in ((0, 32), (32, 60)):
+            tt(V("ff", lo, hi), V("ft", lo, hi), V(a, lo, hi), OP.add)
+        for lo, hi in ((0, 32), (32, 60)):
+            cp(V(off, lo, hi), V("ff", lo, hi))
 
     def hand(off, down):
         def move(a, n, d):
@@ -410,18 +412,52 @@ def rank_program(g, core, T, topo):
             cur = nxt
         return cur
 
+    def short(off, order, cl, down, last, first, beside):
+        beside = iter(beside + [[]] * 6)
+
+        def side():
+            for f in next(beside):
+                f()
+        moves = hand(off, down)
+        if first:
+            act(R("ra"), IDENT, AF.Copy, 1.0, None, V(off, order[0], order[0] + 20))
+        else:
+            gather("ra", "ident", off, order[0])
+        if first:
+            first()
+        for f in moves[:2 if first else 3]:
+            f()
+        gather("two", "ra", off, order[1])
+        if first:
+            moves[2]()
+        act(R("ra"), R("two"), AF.Copy, 1.0, None, V(off, order[2], order[2] + 20))
+        act(V("rb", 96, C), R("ra"), AF.Copy, 1.0, None, V(off, order[3] + 6, order[3] + 20))
+        turn("two")
+        side()
+        ts(V("pc", 0, 32), TURNED, 160.0, None, OP.add, None, V(cl, 0, 2))
+        side()
+        for d in (2, 3):
+            n = 128 - 32 * d
+            f, t = (0, 32 * d) if down else (32 * d, 0)
+            cp(V(off, 20 + 40 * d, 40 + 40 * d, 1, t, t + n), V("pc", 0, 20, 1, f, f + n))
+        cp(V("rb", 0, 96), R("ra"), V(off, order[3], order[3] + 6))
+        side()
+        gather("ra", "rb", off, 100)
+        side()
+        gather(last, "ra", off, 140)
+        side()
+
     def inverse():
         op("v", lambda: g.vector.tensor_copy(T.br[:, PAD:PAD + C].indirect(T.ql[:, 0:20]), ap(IDENT)), [IDENT, W("ql")], [R("br")])
-        ts(V("offb", 20, 180), V("i160", 0, 160), L16, None, OP.add)
+        pads("mn")
         turn("br")
         entries("n0l", 160.0)
         cp(V("za", 0, 64), TURNED, V("clb", 0, 4))
         cp(R("mn"), R("mr"), W("n0l"))
-        entries("n0w", 160.0)
+        cp(W("n0w"), W("n0l"))
         turn("mn")
         entries("mnw", 160.0)
         cp(V("zc", 0, 64), TURNED, V("clb", 0, 4))
-        pads("wrb")
 
     def send(rnd, k):
         hm, partner = "hm%d" % rnd, T.cores[rank ^ STEP[rnd]]
@@ -465,11 +501,17 @@ def rank_program(g, core, T, topo):
         if rnd:
             halves("x%d" % rnd)
         places("kn", phi, "clo", "do", "ao", "offo", rnd == 0)
-        moves = hand("offo", True)
-        chain("offo", [0, 20, 80, 60, 120, 100, 160, 140], "wra", [moves[:2], moves[2:], [], [], [], [], [] if rnd else [inverse]],
-              [] if rnd else range(2, 7))
+        if rnd == 0:
+            moves = hand("offo", True)
+            chain("offo", [0, 20, 80, 60, 120, 100, 160, 140], "wra", [moves[:2], moves[2:], [], [], [], [], [inverse]], range(2, 7))
+        else:
+            short("offo", [0, 20, 80, 60], "clo", True, "wra", None, [])
         turn("wra")
+        if rnd == 0:
+            ts(V("offb", 20, 180), V("i160", 0, 160), L16, None, OP.add)
         entries("aoff", 160.0)
+        if rnd == 0:
+            pads("wrb")
         dma("y", "ashs%d" % rnd, T.ash[16:128, 0:C], T.wra[0:112, PAD:PAD + C], [V("wra", PAD, PAD + C, 1, 0, 112)], [V("ash", 0, C, 1, 16, 128)])
         for k in (96, 112):
             dma("y", "a8s%d" % rnd, T.a8[k:k + 16, 0:20], T.aoff[112:128, 0:20], [V("aoff", 0, 20, 1, 112, 128)], [V("a8", 0, 20, 1, k, k + 16)])
@@ -489,33 +531,32 @@ def rank_program(g, core, T, topo):
             tt(W("kap"), W("n0w"), W("mnw"), OP.min)
             table("db", "ab", EVEN, "wo")
             cp(W("kxb"), W("kap"))
+            pads("two")
+        if rnd == 2:
+            turn("cum")
+            tt(V("c1w", 0, 32), TURNED, V("dm", 0, 32), OP.mult, V("own", 0, 2))
         places("kxb", phi and "phb", "clb", "db", "ab", "offb", False)
         if rnd == 0:
             dma("y", "dv", T.vt[:], T.v[:], [], [V("vt", 0, 512)])
         spread = [lambda q=q: cp(V("a8", 0, 20, 1, 32 * q, 32 * q + 32), V("a8", 0, 20, 1, 96, 128)) for q in range(3)]
-        extra = [[[lambda b=b: qz("em", 128 * b, 128 * b + 128, "et")] for b in range(4)] + [spread[:2], spread[2:] + [lambda: pads("cum")]],
-                 [[lambda: qz("vw", 0, 128, "vt")], [lambda: pads("ee2")], spread[:2], spread[2:],
+        em = [lambda b=b: qz("em", 128 * b, 128 * b + 128, "et") for b in range(4)]
+        extra = [[em[:1], em[1:2], em[2:3], em[3:] + spread[:1], spread[1:]],
+                 [[lambda: qz("vw", 0, 128, "vt")], spread[:2], spread[2:] + [lambda: pads("ee2")], [lambda: pads("cum"), lambda: fill(C160, 160.0)],
                   [lambda: fill(V("dm", 20, 32), 0.0), lambda: tt(W("dm"), W("gmi"), W("wi"), OP.subtract)]],
-                 [spread[:2], spread[2:]]][rnd]
-        moves = hand("offb", False)
-        cur = chain("offb", [0, 40, 60, 80, 100, 120, 140, 160], None, [moves[:2] + [lambda: send(rnd, 0)], moves[2:]] + extra, [0])
-        gather("wrb", cur, "a8")
+                 [spread[:2], spread[2:], [lambda: tt(W("fw"), W("c1w"), W("wi"), OP.add)],
+                  [lambda: ts(V("c1w", 0, 32), V("c1w", 0, 32), -2.0, None, OP.mult)],
+                  [lambda: tt(V("dm", 0, 32), V("dm", 0, 32), V("c1w", 0, 32), OP.add)]]][rnd]
+        short("offb", [0, 40, 60, 80], "clb", False, "rb", lambda: send(rnd, 0), extra)
+        gather("wrb", "rb", "a8")
         turn("wrb")
         same(rnd, 0)
         entries("boff", 160.0)
         same(rnd, 1)
         way = _relays(topo, partner, core) or [partner, partner]
         M["arrived"]("t", "arr%d" % rnd, len(SENDS[rnd]) * sum(_count(topo.mask(k, core)) for k in way))
-        for j in range(4):
-            mm("ps%d" % j, "em", 128 * j, land, 0, C)
-            act(V("dsb", C * j, C * j + C), V("ps%d" % j, 0, C))
-        if rnd == 1:
-            tt(R("cum"), R("ee0"), R("ee1"), OP.is_equal)
-            turn("cum")
-            tt(V("c1w", 0, 32), TURNED, V("dm", 0, 32), OP.mult, V("own", 0, 2))
-            tt(W("fw"), W("c1w"), W("wi"), OP.add)
-            ts(V("c1w", 0, 32), V("c1w", 0, 32), -2.0, None, OP.mult)
-            tt(V("dm", 0, 32), V("dm", 0, 32), V("c1w", 0, 32), OP.add)
+        for ps, j, a, b in [(0, 0) + PARTS[0], (4, 0) + PARTS[1]] + [(j, j, 0, C) for j in range(1, 4)]:
+            mm("ps%d" % ps, "em", 128 * j, land, a, b)
+            act(V("dsb", C * j + a, C * j + b), V("ps%d" % ps, 0, b - a))
         summed(Y, "dsb", lambda j, a, b: V("vv", 4 * a + j, 4 * b, 4), "boff")
         for k, (a, b) in enumerate(PARTS):
             qz("xm", a, b, Y)
@@ -524,6 +565,8 @@ def rank_program(g, core, T, topo):
             else:
                 mm("ps%d" % (4 + k), "vw", 0, "xm", a, b)
                 act(V("yt", a, b), V("ps%d" % (4 + k), 0, b - a))
+        if rnd == 1:
+            tt(R("cum"), R("ee0"), R("ee1"), OP.is_equal)
     dma("y", "oend", T.oc[:, 0:4 * C], T.xmq[:, 0:C].bitcast(dt.uint8), [R("xmq")], [])
     dma("s", "oend", T.y[:], T.yt[:], [R("yt")], [])
     for k in range(4):
@@ -532,6 +575,7 @@ def rank_program(g, core, T, topo):
     tt(V("e2w", 0, 32), TURNED, V("dm", 0, 32), OP.mult, V("own", 0, 2))
     tt(W("fw"), W("fw"), W("e2w"), OP.add)
     cp(W("qoff"), W("fw"))
-    ts(R("qf"), R("ar"), 160.0, None, OP.add, None, W("qoff"))
+    act(V("qf", 160, C), R("ar"), AF.Identity, 1.0, C160, V("qoff", 10, 20))
+    ts(V("qf", 0, 160), R("ar"), 160.0, None, OP.add, None, V("qoff", 0, 10))
     dma("y", "oend", T.qo[:], T.qf[0:128:16, 0:C], [R("qf")], [])
     M["finish"]()

@@ -4,13 +4,13 @@ from concourse.mybir import dt, AluOpType, ActivationFunctionType
 C, N = 320, 8
 STEP = [4, 1, 2]
 PARTS = [(0, 192), (192, 320)]
-SENDS = [[(0, C)]] * 3
 PAD = 16
-PADDED = ("ar", "br", "mn", "tin", "wra", "wrb", "ee2", "cum", "two")
+PADDED = ("tab", "two", "wra", "inv", "wrb")
+NEXT, FAR = 64, (104, 148)
 OP, AF = AluOpType, ActivationFunctionType
 
 SCRATCH = {}
-SEMAPHORES = ["cv", "cs", "ct", "cg", "sent", "rarr0", "rsent", "dq", "dm", "dx", "du", "dw", "dv", "oend"]
+SEMAPHORES = ["cv", "cs", "ct", "cg", "sent", "rarr0", "rsent", "dq", "dm", "dx", "du", "dw", "dv", "dk", "oend"]
 
 
 def _declare():
@@ -31,38 +31,38 @@ def _declare():
     mx("vw", 128)
     mx("wm", 512)
     mx("em", 512)
-    for n in ("ut", "vt", "ones"):
+    for n in ("ut", "vt"):
         sb(n, 512, "bfloat16")
-    sb("et", 2048, "bfloat16")
-    for n in ("ident", "mr", "ee0", "ee1", "phb", "sg", "ash", "ak", "ra", "rb"):
+    for n in ("ones", "et"):
+        sb(n, 516, "bfloat16")
+    for n in ("ident", "mix", "ar", "br", "mr", "kr", "ah", "bh", "nh", "mh", "ee", "fo", "fb", "sg", "ash", "ra", "rb"):
         sb(n, C, "bfloat16")
-    for n in PADDED:
-        sb(n, C + 2 * PAD, "bfloat16")
-    sb("turned", 2 * C + 2 * PAD, "bfloat16")
+    for n in ("do", "db", "mo", "mb", "ys", "mq"):
+        sb(n, C, "float16")
+    sb("rows", PAD + len(PADDED) * (C + PAD), "bfloat16")
+    sb("turned", 2 * C + 2 * PAD + 20, "bfloat16")
+    sb("odd", 2 * C, "bfloat16")
     for n in ("xh", "xi", "dsb", "x0", "x1", "x2", "vv", "hh"):
         sb(n, 4 * C, "bfloat16")
     for n in ("qf", "yt"):
         sb(n, C, "float32")
-    sb("i160", 160, "float32")
-    for n in ("za", "zc", "do", "ao", "db", "ab", "ft", "ff"):
-        sb(n, 64, "float32")
-    for n in ("w16", "wi", "we", "wo", "kap", "fw", "t20"):
+    sb("i80", 80, "float32")
+    for n in ("w16", "wi", "kap"):
         sb(n, 20, "float32")
-    for n in ("c1w", "e2w", "n0w", "mnw", "dm"):
-        sb(n, 32, "float32")
+    sb("t32", 32, "float32")
     sb("cols", 16, "float32")
     for n in ("gqi", "gmi"):
         sb(n, 20, "int32")
     sb("ints", 4, "int32")
-    for n in ("ql", "ml", "kn", "kxb", "a8", "qoff"):
+    for n in ("ql", "ml", "kn", "a8"):
         sb(n, 20, "uint16")
-    for n in ("aoff", "boff", "n0l", "pc"):
+    for n in ("aoff", "boff", "n0l", "kxb", "pc"):
         sb(n, 32, "uint16")
     for n in ("clo", "clb", "own"):
         sb(n, 4, "uint16")
     for n in ("offo", "offb"):
-        sb(n, 180, "uint16")
-    for k in range(6):
+        sb(n, 188, "uint16")
+    for k in range(8):
         SCRATCH["ps%d" % k] = ("psum", [128, 512], "float32")
 
 
@@ -75,11 +75,21 @@ def _relays(topo, src, dst):
     c = [k for k in topo.cores_of(src) if topo.may_write(k, dst)]
     same = [k for k in c if topo.die(k) == topo.die(src)]
     other = [k for k in c if topo.die(k) != topo.die(src)]
-    return [same[0], other[0], same[1]]
+    return [other[0], same[0], same[1]]
 
 
 def _count(mask):
     return bin(mask).count("1")
+
+
+def _pieces(topo, src, way):
+    e = topo.engines(src, way[1])
+    half = [sum(1 << x for x in e[len(e) // 2 * i:len(e) // 2 * (i + 1)]) for i in range(2)]
+    return [("q",) + PARTS[0] + (topo.mask(src, way[0]),), ("q",) + PARTS[1] + (half[0],), ("s", 0, C, half[1])]
+
+
+def _view(T, name, a, b):
+    return T[name][:, a:b].bitcast(dt.uint8) if name.endswith("q") else T[name][:, a:b]
 
 
 def V(name, lo, hi, step=1, p0=0, p1=128):
@@ -191,17 +201,11 @@ def _relay_program(g, core, T, topo):
                 continue
             i = way.index(core)
             rid, pid = topo.addr(dst, core)
-            m, e = topo.mask(core, dst), _count(topo.mask(src, core))
-            lq, ls, arr = T["land%dq" % s], T["land%ds" % s], T.sem["arr%d" % s]
-            for k, (lo, hi) in enumerate(SENDS[s]):
-                if i < 2:
-                    a, b = lo + (hi - lo) // 2 * i, lo + (hi - lo) // 2 * (i + 1)
-                    g.wait_ge(T.sem["rarr%d" % k], e // 2)
-                    g.remote_dma(lq[:, a:b].bitcast(dt.uint8), T.relq[:, a:b].bitcast(dt.uint8), arr, T.sem.rsent, pid, rid, m)
-                else:
-                    g.wait_ge(T.sem["rarr%d" % k], e)
-                    g.remote_dma(ls[:, lo:hi], T.rels[:, lo:hi], arr, T.sem.rsent, pid, rid, m)
-            g.wait_ge(T.sem.rsent, len(SENDS[s]) * _count(m))
+            m = topo.mask(core, dst)
+            n, a, b, e = _pieces(topo, src, way)[i]
+            g.wait_ge(T.sem.rarr0, _count(e))
+            g.remote_dma(_view(T, "land%d%s" % (s, n), a, b), _view(T, "rel" + n, a, b), T.sem["arr%d" % s], T.sem.rsent, pid, rid, m)
+            g.wait_ge(T.sem.rsent, _count(m))
 
 
 def rank_program(g, core, T, topo):
@@ -232,12 +236,11 @@ def rank_program(g, core, T, topo):
         else:
             op("v", lambda: g.vector.tensor_scalar(ap(out), src(a, off), k1, k2, o0, o1), rd(a, s1, s2, off), [out])
 
-    def act(out, inn, func=AF.Copy, scale=1.0, bias=None, off=None):
-        k = ap(scale) if isinstance(scale, tuple) else scale
+    def act(out, inn, scale=1.0, off=None, bias=None):
         if bias is None:
-            op("s", lambda: g.scalar.activation(ap(out), src(inn, off), func, scale=k), rd(inn, scale, off), [out])
+            op("s", lambda: g.scalar.activation(ap(out), src(inn, off), AF.Copy, scale=scale), rd(inn, off), [out])
         else:
-            op("s", lambda: g.scalar.activation(ap(out), src(inn, off), func, bias=ap(bias), scale=k), rd(inn, scale, bias, off), [out])
+            op("s", lambda: g.scalar.activation(ap(out), src(inn, off), AF.Identity, bias=ap(bias), scale=scale), rd(inn, bias, off), [out])
 
     def fill(r, c):
         op("v", lambda: g.vector.memset(ap(r), c), [], [r])
@@ -245,8 +248,9 @@ def rank_program(g, core, T, topo):
     def tr(out, inn):
         op("v", lambda: g.vector.transpose(ap(out), ap(inn)), [inn], [out])
 
-    def qz(n, lo, hi, tile):
-        q, s, inn = V(n + "q", lo, hi), V(n + "s", lo, hi), V(tile, 4 * lo, 4 * hi)
+    def qz(n, lo, hi, tile, at=None):
+        at = 4 * lo if at is None else at
+        q, s, inn = V(n + "q", lo, hi), V(n + "s", lo, hi), V(tile, at, at + 4 * (hi - lo))
         op("v", lambda: g.vector.quantize_mx(ap(q), ap(s), ap(inn)), [inn], [q, s])
 
     def mm(ps, a, alo, b, lo, hi):
@@ -262,30 +266,43 @@ def rank_program(g, core, T, topo):
     def sel(out, inn, pattern, o, base, cm):
         op("g", lambda: g.affine_select(ap(out), ap(inn), pattern, o, 0.0, base, cm), [inn], [out])
 
-    def R(n):
-        return V(n, PAD, PAD + C) if n in PADDED else V(n, 0, C)
+    def R(n, lo=0, hi=C, p0=0, p1=128):
+        if n in PADDED:
+            at = PAD + PADDED.index(n) * (C + PAD)
+            return V("rows", at + lo, at + hi, 1, p0, p1)
+        return V(n, lo, hi, 1, p0, p1)
 
     def W(n):
         return V(n, 0, 20)
 
-    L16, ODD, EVEN, H1, HH, HO, T1, C160 = [V("cols", k, k + 1) for k in range(8)]
-    TURNED = V("turned", 0, 2 * C + 2 * PAD)
+    L16, ODD, EVEN, H1, HH, HO, T1, K1, LESS, HALF = [V("cols", k, k + 1) for k in range(10)]
+    STILL = 2 * C + 2 * PAD
+    TURNED = V("turned", 0, STILL + 20)
 
-    def gather(out, win, off, o=0):
-        lo = R(out)[1]
-        act(V(out, lo + 160, lo + C), R(win), AF.Copy, 1.0, None, V(off, o + 10, o + 20))
-        cp(V(out, lo, lo + 160), R(win), V(off, o, o + 10))
+    def pick(out, win, off, o, lo, hi, scalar):
+        a = (R(out, 16 * lo, 16 * hi), R(win))
+        if scalar:
+            act(a[0], a[1], 1.0, V(off, o + lo, o + hi))
+        else:
+            cp(a[0], a[1], V(off, o + lo, o + hi))
 
-    def pads(n):
-        fill(V(n, 0, PAD), 0.0)
-        fill(V(n, PAD + C, 2 * PAD + C), 0.0)
+    def gather(out, win, off, o=0, cut=10, first=()):
+        pick(out, win, off, o, cut, 20, True)
+        for f in first:
+            f()
+        pick(out, win, off, o, 0, cut, False)
 
-    def turn(row):
-        tr(V("turned", 0, C), R(row))
-        tr(V("turned", C, 2 * C + 2 * PAD), V(row, 0, C + 2 * PAD))
+    def pad(k):
+        fill(V("rows", k * (C + PAD), k * (C + PAD) + PAD), 0.0)
 
-    def entries(out, base):
-        ts(V(out, 0, 32), TURNED, base, None, OP.add, None, V("own", 0, 2))
+    def turn(row, cuts=(0, C)):
+        for lo, hi in zip(cuts, cuts[1:]):
+            more = 2 * PAD * (hi == C)
+            tr(V("turned", lo, hi), R(row, lo, hi))
+            tr(V("turned", C + lo, C + hi + more), R(row, lo - PAD, hi - PAD + more))
+
+    def entries(out, cl, lo, hi):
+        ts(V(out, 0, 16 * (hi - lo)), TURNED, 160.0, None, OP.add, None, V(cl, lo, hi))
 
     dma("y", "dq", T.gqi[:], T.gq[:], [], [W("gqi")])
     dma("s", "dm", T.gmi[:], T.gm[:], [], [W("gmi")])
@@ -299,15 +316,11 @@ def rank_program(g, core, T, topo):
     iota(pid, [[1, 1]], 0, 1, False)
     iota(W("w16"), [[16, 20]], 0, 0)
     iota(IDENT, [[1, C]], -160, 0)
-    iota(V("i160", 0, 160), [[0, 8], [16, 20]], 0, 0)
-    iota(V("ones", 0, 512), [[0, 512]], 1, 0)
-
-    def unpacker(b):
-        sel(V("et", 512 * b, 512 * b + 512), V("ones", 0, 512), [[1, 128], [1000, 4]], OP.is_equal, -1000 * b, -1)
-    unpacker(0)
-    unpacker(1)
-    for n in ("ar", "br", "tin", "wra"):
-        pads(n)
+    iota(R("mix"), [[1, C]], -160, 0)
+    iota(V("i80", 0, 80), [[0, 4], [16, 20]], 0, 0)
+    iota(V("ones", 0, 516), [[0, 516]], 1, 0)
+    sel(V("et", 0, 516), V("ones", 0, 516), [[1, 516]], OP.is_equal, -3, -4)
+    iota(R("ash"), [[1, C]], -160, 0)
     ts(i0, pid, 15, None, OP.bitwise_and)
     ts(i1, pid, 4, 1, OP.arith_shift_right, OP.bitwise_and)
     ts(i2, pid, 1, None, OP.bitwise_and)
@@ -318,246 +331,231 @@ def rank_program(g, core, T, topo):
     ts(W("wi"), W("w16"), L16, None, OP.add)
     ts(HH, T1, ODD, H1, OP.mult, OP.add)
     ts(EVEN, i1, -1.0, 1.0, OP.mult, OP.add)
-    J, J16, B1, B2, B3 = V("wi", 0, 4), V("t20", 0, 4), V("t20", 4, 8), V("t20", 8, 12), V("t20", 12, 16)
+    J = V("wi", 0, 4)
+    J16, B1, B2, B3, Z, U, F1, F2 = [V("t32", 4 * k, 4 * k + 4) for k in range(8)]
     ts(J16, J, 59.0, 16.0, OP.min, OP.mult)
-    ts(B2, J, 40.0, -304.0, OP.is_ge, OP.mult)
-    ts(B1, J, 20.0, -336.0, OP.is_ge, OP.mult)
+    ts(B1, J, 20.0, -320.0, OP.is_ge, OP.mult)
+    ts(B2, J, 40.0, -320.0, OP.is_ge, OP.mult)
+    ts(K1, HH, -1.0, float(STILL), OP.mult, OP.add)
     ts(HO, ODD, 16.0, HH, OP.mult, OP.add)
-    tt(J16, J16, B2, OP.add)
+    tt(J16, J16, B1, OP.add)
     ts(B3, J, 19.0, 16.0, OP.min, OP.mult)
-    tt(B2, J16, B1, OP.add)
-    ts(V("own", 0, 2), V("t20", 12, 14), HO, None, OP.add)
-    ts(V("clo", 0, 4), B2, HH, 16.0, OP.add, OP.add)
-    ts(W("we"), W("wi"), EVEN, None, OP.mult)
-    ts(V("offo", 20, 180), V("i160", 0, 160), L16, None, OP.add)
+    ts(U, J, -15.0, K1, OP.mult, OP.add)
+    tt(J16, J16, B2, OP.add)
+    ts(Z, J, 20.0, None, OP.is_lt)
+    ts(B2, J, 40.0, 16.0, OP.is_ge, OP.mult)
+    ts(V("own", 0, 2), V("t32", 12, 14), HO, None, OP.add)
+    ts(F1, U, EVEN, None, OP.mult)
+    ts(V("turned", STILL, STILL + 20), W("wi"), -160.0, None, OP.add)
+    tt(B1, J16, B2, OP.add)
+    tt(F1, F1, Z, OP.mult)
+    ts(F2, U, -16.0, ODD, OP.add, OP.mult)
+    tt(B1, B1, F1, OP.add)
     cp(W("ql"), W("gqi"))
     cp(W("ml"), W("gmi"))
-    gather("ar", "ident", "ql")
     tt(W("kap"), W("gmi"), W("wi"), OP.min)
-    act(R("br"), R("ar"), AF.Copy, 1.0, None, W("ml"))
+    gather("ar", "ident", "ql")
     cp(W("kn"), W("kap"))
-    act(R("mr"), IDENT, AF.Copy, 1.0, None, W("ml"))
-
-    def table(d, a, keep, idle):
-        ts(W("fw"), W("za"), 160.0, keep, OP.add, OP.mult)
-        tt(V(d, 0, 64), V("zc", 0, 64), V("za", 0, 64), OP.subtract)
-        ts(V(a, 20, 64), V("za", 20, 64), 160.0, None, OP.add)
-        tt(W(a), W("fw"), W(idle), OP.add)
-        ts(W(d), W(d), keep, None, OP.mult)
+    act(R("br"), R("ar"), 1.0, W("ml"))
+    act(R("kr"), IDENT, 1.0, W("kn"))
+    dma("y", "dk", T.mix[1:128:16, 0:C], T.kr[1:128:16, 0:C], [R("kr")], [R("mix")])
+    dma("y", "dv", T.vt[:], T.v[:], [], [V("vt", 0, 512)])
+    act(R("mr"), IDENT, 1.0, W("ml"))
+    ts(V("clo", 0, 4), B1, HH, None, OP.add)
+    pad(0)
+    pad(1)
 
     def halves(X):
         for b in range(4):
-            act(V("xh", C * b, C * b + C), V(X, b, 4 * C, 4), AF.Copy, 0.5)
-            sel(V("xi", C * b, C * b + C), V("xh", C * b, C * b + C), [[0, C]], OP.is_gt, 1, 0)
+            act(V("xh", C * b, C * b + C), V(X, b, 4 * C, 4), 0.5)
+            o = V("xi", 2 * C + b // 2, 4 * C, 2) if b % 2 else V("xi", C * b // 2, C * b // 2 + C)
+            sel(o, V("xh", C * b, C * b + C), [[0, C]], OP.is_gt, 1, 0)
 
     def scores(xm, k):
         mm("ps%d" % (4 + k), "u2", 0, xm, PARTS[k][0], PARTS[k][1])
 
-    turn("ar")
-    ts(B1, J, 20.0, -320.0, OP.is_ge, OP.mult)
-    cp(V("za", 0, 64), TURNED, V("clo", 0, 4))
-    ts(W("wo"), W("wi"), ODD, None, OP.mult)
-    tt(B2, J16, B1, OP.add)
+    def still(off, lo, hi):
+        ts(V(off, lo, hi), V("i80", 0, hi - lo), L16, None, OP.add)
+
     qz("u2", 0, 128, "ut")
     for k, (a, b) in enumerate(PARTS):
         qz("xm", a, b, "x0")
         scores("xm", k)
     halves("x0")
-    unpacker(2)
-    unpacker(3)
-    turn("br")
-    ts(V("clb", 0, 4), B2, HH, None, OP.add)
+    tt(R("do"), R("br"), R("ar"), OP.subtract)
 
-    def places(kx, phi, cl, d, a, off, shared):
-        for k, (lo, hi) in enumerate(PARTS):
-            ts(V("sg", lo, hi), V("ps%d" % (4 + k), 0, hi - lo), 0.0, None, OP.is_gt)
-        if shared:
-            cp(V("zc", 0, 64), TURNED, V(cl, 0, 4))
-            gather("tin", "sg", kx)
-            table(d, a, ODD, "we")
-            turn("tin")
-        else:
-            for h in range(2):
-                o, l = V("tin", PAD + 160 * h, PAD + 160 * h + 160), V(kx, 10 * h, 10 * h + 10)
-                if phi:
-                    tt(o, R("sg"), V(phi, R(phi)[1] + 160 * h, R(phi)[1] + 160 * h + 160), OP.is_equal, l)
-                else:
-                    cp(o, R("sg"), l)
-            for lo, hi in ((0, 160), (160, C)):
-                tr(V("turned", lo, hi), V("tin", PAD + lo, PAD + hi))
-                tr(V("turned", C + lo, C + hi + 2 * PAD * (lo > 0)), V("tin", lo, hi + 2 * PAD * (lo > 0)))
-        for h in range(2):
-            tt(V("ft", 32 * h, 32 * h + 32), TURNED, V(d, 32 * h, 32 * h + 32), OP.mult, V(cl, 2 * h, 2 * h + 2))
-        for lo, hi in ((0, 32), (32, 60)):
-            tt(V("ff", lo, hi), V("ft", lo, hi), V(a, lo, hi), OP.add)
-        for lo, hi in ((0, 32), (32, 60)):
-            cp(V(off, lo, hi), V("ff", lo, hi))
-
-    def hand(off, down):
-        def move(a, n, d):
-            f, t = (a, a + 32 * d) if down else (128 - a - n, 128 - a - n - 32 * d)
-            return lambda: cp(V(off, 20 + 40 * d, 20 + 80 * d, 1, t, t + n), V(off, 20, 20 + 40 * d, 1, f, f + n))
-        return [move(0, 32, 1), move(32, 32, 1), move(64, 32, 1), move(0, 64, 2)]
-
-    def chain(off, order, last, beside, solo):
-        cur = "ident"
-        for n, o in enumerate(order):
-            nxt = last if last and n == 7 else ("ra", "rb")[n % 2]
-            if n in solo:
-                act(R(nxt), R(cur), AF.Copy, 1.0, None, V(off, o, o + 20))
-            else:
-                gather(nxt, cur, off, o)
-            for f in (beside + [[]] * 8)[n]:
+    def places(kx, d, a, cl, off, first, between):
+        def side(k):
+            for f in between[k]:
                 f()
-            cur = nxt
-        return cur
+        for k, (lo, hi) in enumerate(PARTS):
+            if first:
+                ts(V("sg", lo, hi), V("ps%d" % (4 + k), 0, hi - lo), 0.0, None, OP.is_gt)
+            else:
+                ts(V("sg", lo, hi), V("ps%d" % (4 + k), 0, hi - lo), 0.0, 0.5, OP.is_gt, OP.subtract)
+        side(0)
+        for h in range(2):
+            tt(R("ys", 160 * h, 160 * h + 160), R("sg"), R(d, 160 * h, 160 * h + 160), OP.mult, V(kx, 10 * h, 10 * h + 10))
+        for h in range(2):
+            tt(R("tab", 160 * h, 160 * h + 160), R("ys", 160 * h, 160 * h + 160), R(a, 160 * h, 160 * h + 160), OP.add)
+        side(1)
+        turn("tab", (0, 160, C))
+        side(2)
+        entries(off, cl, 0, 4)
+        side(3)
 
-    def short(off, order, cl, down, last, first, beside):
-        beside = iter(beside + [[]] * 6)
+    def move(off, down, a, n, d, at, lo, hi, frm=None):
+        f, t = (a, a + 32 * d) if down else (128 - a - n, 128 - a - n - 32 * d)
+        return lambda: cp(V(off, at, at + hi - lo, 1, t, t + n), V(frm or off, lo, hi, 1, f, f + n))
+
+    def chain(off, cl, down, last, far, cut, beside):
+        beside = iter(beside + [[]] * 5)
 
         def side():
             for f in next(beside):
                 f()
-        moves = hand(off, down)
-        if first:
-            act(R("ra"), IDENT, AF.Copy, 1.0, None, V(off, order[0], order[0] + 20))
-        else:
-            gather("ra", "ident", off, order[0])
-        if first:
-            first()
-        for f in moves[:2 if first else 3]:
-            f()
-        gather("two", "ra", off, order[1])
-        if first:
-            moves[2]()
-        act(R("ra"), R("two"), AF.Copy, 1.0, None, V(off, order[2], order[2] + 20))
-        act(V("rb", 96, C), R("ra"), AF.Copy, 1.0, None, V(off, order[3] + 6, order[3] + 20))
+        gather("two", "tab", off, 0, cut, [move(off, down, a, 32, 1, NEXT, 20, 60) for a in (0, 32, 64)])
+        pick("ra", "two", off, NEXT + 20, 0, 20, True)
+        pick("rb", "ra", off, NEXT, 6, 20, True)
+        side()
         turn("two")
         side()
-        ts(V("pc", 0, 32), TURNED, 160.0, None, OP.add, None, V(cl, 0, 2))
+        entries("pc", cl, 2, 4)
         side()
         for d in (2, 3):
-            n = 128 - 32 * d
-            f, t = (0, 32 * d) if down else (32 * d, 0)
-            cp(V(off, 20 + 40 * d, 40 + 40 * d, 1, t, t + n), V("pc", 0, 20, 1, f, f + n))
-        cp(V("rb", 0, 96), R("ra"), V(off, order[3], order[3] + 6))
+            move(off, down, 0, 128 - 32 * d, d, far[d - 2], 8, 28, "pc")()
+        pick("rb", "ra", off, NEXT, 0, 6, False)
         side()
-        gather("ra", "rb", off, 100)
+        gather("ra", "rb", off, far[0])
         side()
-        gather(last, "ra", off, 140)
-        side()
+        gather(last, "ra", off, far[1])
 
-    def inverse():
-        op("v", lambda: g.vector.tensor_copy(T.br[:, PAD:PAD + C].indirect(T.ql[:, 0:20]), ap(IDENT)), [IDENT, W("ql")], [R("br")])
-        pads("mn")
-        turn("br")
-        entries("n0l", 160.0)
-        cp(V("za", 0, 64), TURNED, V("clb", 0, 4))
-        cp(R("mn"), R("mr"), W("n0l"))
-        cp(W("n0w"), W("n0l"))
-        turn("mn")
-        entries("mnw", 160.0)
-        cp(V("zc", 0, 64), TURNED, V("clb", 0, 4))
+    def long_chain():
+        gather("two", "tab", "offo", 0, 6, [move("offo", True, a, 32, 1, NEXT, 20, 60) for a in (0, 32, 64)])
+        move("offo", True, 0, 64, 2, FAR[0], 20, FAR[0])()
+        cur = "two"
+        for n, o in enumerate([NEXT + 20, NEXT, FAR[0] + 20, FAR[0], FAR[1] + 20]):
+            pick(("ra", "rb")[n % 2], cur, "offo", o, 0, 20, True)
+            cur = ("ra", "rb")[n % 2]
+        pad(3)
+        pad(4)
+        w = R("inv")
+        op("v", lambda: g.vector.tensor_copy(ap(w).indirect(T.ql[:, 0:20]), ap(R("mix"))), [R("mix"), W("ql")], [w])
+        ts(V("own", 2, 4), V("t32", 12, 14), HO, 1.0, OP.add, OP.add)
+        turn("inv")
+        qz("em", 0, 128, "et", 3)
+        entries("n0l", "own", 0, 2)
+        entries("kxb", "own", 2, 4)
+        tt(R("db"), R("mr"), w, OP.subtract, W("n0l"))
+        for b in range(1, 4):
+            qz("em", 128 * b, 128 * b + 128, "et", 3 - b)
+        qz("vw", 0, 128, "vt")
+        gather("wra", cur, "offo", FAR[1])
 
     def send(rnd, k):
         hm, partner = "hm%d" % rnd, T.cores[rank ^ STEP[rnd]]
-        hq, hs = T[hm + "q"], T[hm + "s"]
-        lo, hi = SENDS[rnd][k]
-        qz(hm, lo, hi, "hh")
-        M["deps"]("g", [V(hm + "q", lo, hi), V(hm + "s", lo, hi)], [])
         way = _relays(topo, core, partner)
+        qz(hm, PARTS[k][0], PARTS[k][1], "hh")
         if way:
-            fq, arr = [], T.sem["rarr%d" % k]
-            for i in range(2):
-                a, b = lo + (hi - lo) // 2 * i, lo + (hi - lo) // 2 * (i + 1)
-                rid, p = topo.addr(way[i], core)
-                e = topo.engines(core, way[i])
-                m = sum(1 << x for x in e[len(e) // 2 * i:len(e) // 2 * (i + 1)])
-                fq.append(RemoteDMATransfer(dst_ids=[DstId(rid=rid, pnc=p)], dma_engine_mask=m, remote_sem=arr,
-                                            src=hq[:, a:b].bitcast(dt.uint8), dst=T.relq[:, a:b].bitcast(dt.uint8)))
-            g.remote_dma_fused(fq, local_sem=T.sem.sent)
-            rid, p = topo.addr(way[2], core)
-            m = topo.mask(core, way[2])
-            g.remote_dma(T.rels[:, lo:hi], hs[:, lo:hi], arr, T.sem.sent, p, rid, m)
+            go = [(way[i], "rel", "rarr0", _pieces(topo, core, way)[i]) for i in ([0], [1, 2])[k]]
         else:
-            rid, p = topo.addr(partner, core)
-            m, arr = topo.mask(core, partner), T.sem["arr%d" % rnd]
-            g.remote_dma(T["land%dq" % rnd][:, lo:hi].bitcast(dt.uint8), hq[:, lo:hi].bitcast(dt.uint8), arr, T.sem.sent, p, rid, m)
-            g.remote_dma(T["land%ds" % rnd][:, lo:hi], hs[:, lo:hi], arr, T.sem.sent, p, rid, m)
-        M["cnt"]["sent"] = M["cnt"].get("sent", 0) + 2 * _count(m)
+            m = topo.mask(core, partner)
+            go = [(partner, "land%d" % rnd, "arr%d" % rnd, (n, 0, C, m)) for n in ("", "qs")[k]]
+        for to, land, arr, (n, a, b, m) in go:
+            M["deps"]("g", [V(hm + n, a, b)], [])
+            rid, p = topo.addr(to, core)
+            g.remote_dma(_view(T, land + n, a, b), _view(T, hm + n, a, b), T.sem[arr], T.sem.sent, p, rid, m)
+            M["cnt"]["sent"] = M["cnt"].get("sent", 0) + _count(m)
 
-    def same(rnd, h):
-        lo = R("ee%d" % rnd)[1] + 160 * h
-        tt(V("ee%d" % rnd, lo, lo + 160), R("wrb"), V("ak", 160 * h, 160 * h + 160), OP.is_equal, V("kn", 10 * h, 10 * h + 10))
+    def fourths(out, a, b, o):
+        return [[lambda h=h: tt(R(out, h, h + 80), R(a, h, h + 80), R(b, h, h + 80), o)] for h in range(0, C, 80)]
 
-    def summed(out, win, other, off):
-        for j, a, b in [(0, 0, C), (1, 0, C), (2, 0, C)] + [(3, a, b) for a, b in PARTS]:
-            tt(V(out, 4 * a + j, 4 * b, 4), V(win, C * j, C * j + C), other(j, a, b), OP.add, V(off, a // 16, b // 16))
+    def mean(j, k):
+        a, b = PARTS[k]
+        win, l = V("xh", C * j, C * j + C), V("aoff", a // 16, b // 16)
+        if j % 2:
+            act(V("odd", 2 * a + j // 2, 2 * b, 2), win, 1.0, l)
+        else:
+            tt(V("vv", 4 * a + j, 4 * b, 4), win, V("xi", C * j // 2 + a, C * j // 2 + b), OP.add, l)
+
+    def join(k):
+        a, b = PARTS[k]
+        tt(V("vv", 4 * a + 1, 4 * b, 2), V("odd", 2 * a, 2 * b), V("xi", 2 * C + 2 * a, 2 * C + 2 * b), OP.add)
+
+    def layer(k):
+        a, b = PARTS[k]
+        qz("vm", a, b, "vv")
+        scores("vm", k)
+        for j in range(4):
+            ps = "ps%d" % ((0, 1, 2, 3), (6, 7, 0, 1))[k][j]
+            mm(ps, "wm", 128 * j, "vm", a, b)
+            act(V("hh", 4 * a + j, 4 * b, 4), V(ps, 0, b - a), 0.03125)
 
     for rnd in range(3):
-        Y, hm, land = "x%d" % (1 + rnd % 2), "hm%d" % rnd, "land%d" % rnd
-        phi = (None, "ee0", "cum")[rnd]
+        Y, land = "x%d" % (1 + rnd % 2), "land%d" % rnd
         partner = T.cores[rank ^ STEP[rnd]]
-        if rnd:
-            halves("x%d" % rnd)
-        places("kn", phi, "clo", "do", "ao", "offo", rnd == 0)
         if rnd == 0:
-            moves = hand("offo", True)
-            chain("offo", [0, 20, 80, 60, 120, 100, 160, 140], "wra", [moves[:2], moves[2:], [], [], [], [], [inverse]], range(2, 7))
+            places("kn", "do", "ar", "clo", "offo", True, [[lambda: still("offo", NEXT, NEXT + 80)], [], [lambda: still("offo", FAR[1], FAR[1] + 40)], [lambda: pad(2)]])
+            long_chain()
+            act(R("ah"), R("ar"), 0.5)
+            act(R("bh"), R("br"), 0.5)
         else:
-            short("offo", [0, 20, 80, 60], "clo", True, "wra", None, [])
+            a, b = fourths("mb", "nh", "mh", OP.add) if rnd == 1 else [[]] * 4, fourths("db", "db", "fb", OP.mult)
+            places("kn", "do", "mo", "clo", "offo", False, [a[0], [], a[1], a[2]])
+            chain("offo", "clo", True, "wra", FAR, 6, [a[3]] + b)
         turn("wra")
         if rnd == 0:
-            ts(V("offb", 20, 180), V("i160", 0, 160), L16, None, OP.add)
-        entries("aoff", 160.0)
+            still("offb", NEXT, NEXT + 80)
+        entries("aoff", "own", 0, 2)
         if rnd == 0:
-            pads("wrb")
-        dma("y", "ashs%d" % rnd, T.ash[16:128, 0:C], T.wra[0:112, PAD:PAD + C], [V("wra", PAD, PAD + C, 1, 0, 112)], [V("ash", 0, C, 1, 16, 128)])
+            pad(5)
+            tt(B2, J16, B2, OP.subtract)
+        dma("y", "ashs%d" % rnd, T.ash[16:128:16, 0:C], T.rows[0:112:16, R("wra")[1]:R("wra")[2]], [R("wra")], [R("ash")])
         for k in (96, 112):
             dma("y", "a8s%d" % rnd, T.a8[k:k + 16, 0:20], T.aoff[112:128, 0:20], [V("aoff", 0, 20, 1, 112, 128)], [V("a8", 0, 20, 1, k, k + 16)])
+        for j, k in ((0, 0), (1, 0), (2, 0), (3, 0), (0, 1), (1, 1), (3, 1)):
+            mean(j, k)
+        join(0)
+        mean(2, 1)
+        layer(0)
+        join(1)
         if rnd == 0:
-            act(V("ash", 0, C, 1, 0, 16), V("ident", 0, C, 1, 0, 16))
-        else:
-            act(R("phb"), R(phi), AF.Copy, 1.0, None, W("n0l"))
-        summed("vv", "xh", lambda j, a, b: V("xi", C * j + a, C * j + b), "aoff")
-        for k, (a, b) in enumerate(PARTS):
-            qz("vm", a, b, "vv")
-            scores("vm", k)
-        act(R("ak"), R("ash"), AF.Copy, 1.0, None, W("kn"))
-        for j in range(4):
-            mm("ps%d" % j, "wm", 128 * j, "vm", 0, C)
-            act(V("hh", j, 4 * C, 4), V("ps%d" % j, 0, C), AF.Copy, 0.03125)
+            tt(F2, F2, Z, OP.mult)
+            fill(LESS, -1.0)
+        layer(1)
+        more = [[]] * 4
         if rnd == 0:
-            tt(W("kap"), W("n0w"), W("mnw"), OP.min)
-            table("db", "ab", EVEN, "wo")
-            cp(W("kxb"), W("kap"))
-            pads("two")
-        if rnd == 2:
-            turn("cum")
-            tt(V("c1w", 0, 32), TURNED, V("dm", 0, 32), OP.mult, V("own", 0, 2))
-        places("kxb", phi and "phb", "clb", "db", "ab", "offb", False)
-        if rnd == 0:
-            dma("y", "dv", T.vt[:], T.v[:], [], [V("vt", 0, 512)])
+            act(R("nh"), R("inv"), 0.5)
+            act(R("mh"), R("mr"), 0.5, W("n0l"))
+            tt(B2, B2, F2, OP.add)
+            more = fourths("mo", "ah", "bh", OP.add)
+        if rnd == 1:
+            more = [[lambda h=h: ts(R("mq", h, h + 160), R("mo", h, h + 160), 160.0, None, OP.add)] for h in (0, 160)] + [[lambda: fill(HALF, 0.5)], []]
+        places("kxb", "db", "mb" if rnd else "inv", "clb", "offb", rnd == 0,
+               [[lambda: ts(V("clb", 0, 4), B2, HH, 16.0, OP.add, OP.add)] * (rnd == 0), [], [lambda: send(rnd, 0)], [lambda: send(rnd, 1)]])
         spread = [lambda q=q: cp(V("a8", 0, 20, 1, 32 * q, 32 * q + 32), V("a8", 0, 20, 1, 96, 128)) for q in range(3)]
-        em = [lambda b=b: qz("em", 128 * b, 128 * b + 128, "et") for b in range(4)]
-        extra = [[em[:1], em[1:2], em[2:3], em[3:] + spread[:1], spread[1:]],
-                 [[lambda: qz("vw", 0, 128, "vt")], spread[:2], spread[2:] + [lambda: pads("ee2")], [lambda: pads("cum"), lambda: fill(C160, 160.0)],
-                  [lambda: fill(V("dm", 20, 32), 0.0), lambda: tt(W("dm"), W("gmi"), W("wi"), OP.subtract)]],
-                 [spread[:2], spread[2:], [lambda: tt(W("fw"), W("c1w"), W("wi"), OP.add)],
-                  [lambda: ts(V("c1w", 0, 32), V("c1w", 0, 32), -2.0, None, OP.mult)],
-                  [lambda: tt(V("dm", 0, 32), V("dm", 0, 32), V("c1w", 0, 32), OP.add)]]][rnd]
-        short("offb", [0, 40, 60, 80], "clb", False, "rb", lambda: send(rnd, 0), extra)
+        chain("offb", "clb", False, "rb", (FAR[0], FAR[0] + 20), 4, [more[0], spread[:2], spread[2:], more[1], more[2]])
+        for f in more[3]:
+            f()
         gather("wrb", "rb", "a8")
         turn("wrb")
-        same(rnd, 0)
-        entries("boff", 160.0)
-        same(rnd, 1)
+        tt(R("ee", 0, 160), R("wrb", 0, 160), R("ash", 0, 160), OP.is_equal)
+        entries("boff", "own", 0, 2)
+        tt(R("ee", 160, C), R("wrb", 160, C), R("ash", 160, C), OP.is_equal)
         way = _relays(topo, partner, core) or [partner, partner]
-        M["arrived"]("t", "arr%d" % rnd, len(SENDS[rnd]) * sum(_count(topo.mask(k, core)) for k in way))
+        M["arrived"]("t", "arr%d" % rnd, sum(_count(topo.mask(k, core)) for k in way))
         for ps, j, a, b in [(0, 0) + PARTS[0], (4, 0) + PARTS[1]] + [(j, j, 0, C) for j in range(1, 4)]:
             mm("ps%d" % ps, "em", 128 * j, land, a, b)
             act(V("dsb", C * j + a, C * j + b), V("ps%d" % ps, 0, b - a))
-        summed(Y, "dsb", lambda j, a, b: V("vv", 4 * a + j, 4 * b, 4), "boff")
+        act(V("odd", 0, C), V("dsb", 3 * C, 4 * C), 1.0, W("boff"))
+        if rnd < 2:
+            act(R("fo"), R("ee"), 2.0, W("kn"), LESS)
+        else:
+            act(R("fo"), R("ee"), -1.0, W("kn"), HALF)
+        for j in range(3):
+            tt(V(Y, j, 4 * C, 4), V("dsb", C * j, C * j + C), V("vv", j, 4 * C, 4), OP.add, W("boff"))
+        for a, b in PARTS:
+            tt(V(Y, 4 * a + 3, 4 * b, 4), V("odd", a, b), V("vv", 4 * a + 3, 4 * b, 4), OP.add)
         for k, (a, b) in enumerate(PARTS):
             qz("xm", a, b, Y)
             if rnd < 2:
@@ -565,17 +563,14 @@ def rank_program(g, core, T, topo):
             else:
                 mm("ps%d" % (4 + k), "vw", 0, "xm", a, b)
                 act(V("yt", a, b), V("ps%d" % (4 + k), 0, b - a))
-        if rnd == 1:
-            tt(R("cum"), R("ee0"), R("ee1"), OP.is_equal)
+        tt(R("do"), R("do"), R("fo"), OP.mult)
+        if rnd < 2:
+            act(R("fb"), R("ee"), 2.0, W("kxb"), LESS)
+            halves(Y)
     dma("y", "oend", T.oc[:, 0:4 * C], T.xmq[:, 0:C].bitcast(dt.uint8), [R("xmq")], [])
     dma("s", "oend", T.y[:], T.yt[:], [R("yt")], [])
     for k in range(4):
         dma("y", "oend", T.osc[4 * k:4 * k + 4, 0:C], T.xms[32 * k:32 * k + 4, 0:C], [R("xms")], [])
-    turn("ee2")
-    tt(V("e2w", 0, 32), TURNED, V("dm", 0, 32), OP.mult, V("own", 0, 2))
-    tt(W("fw"), W("fw"), W("e2w"), OP.add)
-    cp(W("qoff"), W("fw"))
-    act(V("qf", 160, C), R("ar"), AF.Identity, 1.0, C160, V("qoff", 10, 20))
-    ts(V("qf", 0, 160), R("ar"), 160.0, None, OP.add, None, V("qoff", 0, 10))
+    tt(R("qf"), R("do"), R("mq"), OP.add)
     dma("y", "oend", T.qo[:], T.qf[0:128:16, 0:C], [R("qf")], [])
     M["finish"]()

from concourse.bass import DstId, RemoteDMATransfer
from concourse.mybir import dt, AluOpType, ActivationFunctionType

C, N = 320, 8
STEP = [4, 1, 2]
PARTS = [(0, 192), (192, 320)]
PAD = 16
PADDED = ("tab", "two", "wra", "inv", "wrb")
NEXT, FAR = 64, (104, 148)
OP, AF = AluOpType, ActivationFunctionType

SCRATCH = {}
SEMAPHORES = ["cv", "cs", "ct", "cg", "sent", "rarr0", "rsent", "dq", "dm", "dx", "du", "dw", "dv", "dk", "oend"]


def _declare():
    def sb(name, n, d):
        SCRATCH[name] = ("sbuf", [128, n], d)

    def mx(name, n):
        sb(name + "q", n, "float8_e4m3fn_x4")
        sb(name + "s", n, "uint8")
    mx("xm", C)
    mx("vm", C)
    for r in range(3):
        mx("hm%d" % r, C)
        mx("land%d" % r, C)
        SEMAPHORES.extend(["arr%d" % r, "a8s%d" % r, "ashs%d" % r])
    mx("rel", C)
    mx("u2", 128)
    mx("vw", 128)
    mx("wm", 512)
    mx("em", 512)
    for n in ("ut", "vt"):
        sb(n, 512, "bfloat16")
    for n in ("ones", "et"):
        sb(n, 516, "bfloat16")
    for n in ("ident", "mix", "ar", "br", "mr", "kr", "ah", "bh", "nh", "mh", "ee", "fo", "fb", "sg", "ash", "ra", "rb"):
        sb(n, C, "bfloat16")
    for n in ("do", "db", "mo", "mb", "ys", "mq"):
        sb(n, C, "float16")
    sb("rows", PAD + len(PADDED) * (C + PAD), "bfloat16")
    sb("turned", 2 * C + 2 * PAD + 20, "bfloat16")
    sb("odd", 2 * C, "bfloat16")
    for n in ("xh", "xi", "dsb", "x0", "x1", "x2", "vv", "hh"):
        sb(n, 4 * C, "bfloat16")
    for n in ("qf", "yt"):
        sb(n, C, "float32")
    sb("i80", 80, "float32")
    for n in ("w16", "wi", "kap"):
        sb(n, 20, "float32")
    sb("t32", 32, "float32")
    sb("cols", 16, "float32")
    for n in ("gqi", "gmi"):
        sb(n, 20, "int32")
    sb("ints", 4, "int32")
    for n in ("ql", "ml", "kn", "a8"):
        sb(n, 20, "uint16")
    for n in ("aoff", "boff", "n0l", "kxb", "pc"):
        sb(n, 32, "uint16")
    for n in ("clo", "clb", "own"):
        sb(n, 4, "uint16")
    for n in ("offo", "offb"):
        sb(n, 188, "uint16")
    for k in range(8):
        SCRATCH["ps%d" % k] = ("psum", [128, 512], "float32")


_declare()


def _relays(topo, src, dst):
    if topo.may_write(src, dst):
        return []
    c = [k for k in topo.cores_of(src) if topo.may_write(k, dst)]
    same = [k for k in c if topo.die(k) == topo.die(src)]
    other = [k for k in c if topo.die(k) != topo.die(src)]
    return [other[0], same[0], same[1]]


def _count(mask):
    return bin(mask).count("1")


def _pieces(topo, src, way):
    e = topo.engines(src, way[1])
    half = [sum(1 << x for x in e[len(e) // 2 * i:len(e) // 2 * (i + 1)]) for i in range(2)]
    return [("q",) + PARTS[0] + (topo.mask(src, way[0]),), ("q",) + PARTS[1] + (half[0],), ("s", 0, C, half[1])]


def _view(T, name, a, b):
    return T[name][:, a:b].bitcast(dt.uint8) if name.endswith("q") else T[name][:, a:b]


def V(name, lo, hi, step=1, p0=0, p1=128):
    return (name, lo, hi, step, p0, p1)


def _machine(g, T):
    eng = {"v": g.vector, "s": g.scalar, "t": g.tensor, "g": g, "y": g.sync}
    cnt, log, snap, closed = {}, {}, {}, set()
    known = {q: {} for q in eng}

    def ap(r):
        n, lo, hi, st, p0, p1 = r
        if st == 1:
            return T[n][p0:p1, lo:hi]
        return T[n][p0:p1, lo:hi:st]

    def hit(a, b):
        if a[1] >= b[2] or b[1] >= a[2] or a[4] >= b[5] or b[4] >= a[5]:
            return False
        if a[3] == b[3] and a[3] > 1 and (a[1] - b[1]) % a[3]:
            return False
        return True

    def learn(q, sem, c):
        k = known[q]
        if k.get(sem, 0) >= c:
            return
        k[sem] = c
        for s, v in snap.get((sem, c), {}).items():
            if k.get(s, 0) < v:
                k[s] = v

    def wait(q, sem, c):
        if known[q].get(sem, 0) >= c:
            return
        if sem not in ("cv", "cs", "ct", "cg"):
            c = cnt[sem]
            closed.add(sem)
        eng[q].wait_ge(T.sem[sem], c)
        learn(q, sem, c)

    def norm(r):
        if r[0].startswith("ps"):
            return (r[0], 0, 512, 1, 0, 128)
        return r

    def deps(q, reads, writes):
        need = {}
        for rs, w in ((reads, False), (writes, True)):
            for r in rs:
                r = norm(r)
                ps = r[0].startswith("ps")
                for (o, ow, oq, sem, c) in log.get(r[0], []):
                    if (w or ow or (ps and oq != q)) and hit(r, o):
                        if need.get(sem, 0) < c:
                            need[sem] = c
        own = known[q]
        for sem in sorted(need, key=lambda s: (s == "c" + q, s)):
            if own.get(sem, 0) < need[sem]:
                wait(q, sem, need[sem])

    def note(q, reads, writes, sem):
        c = cnt[sem]
        s = dict(known[q])
        snap[(sem, c)] = s
        for rs, w in ((reads, False), (writes, True)):
            for r in rs:
                r = norm(r)
                old = log.get(r[0], [])
                if w:
                    old = [e for e in old if not (r[1] <= e[0][1] and e[0][2] <= r[2] and r[3] == 1
                                                  and r[4] <= e[0][4] and e[0][5] <= r[5])]
                log[r[0]] = old + [(r, w, q, sem, c)]

    def op(q, fn, reads, writes):
        deps(q, reads, writes)
        sem = "c" + q
        cnt[sem] = cnt.get(sem, 0) + 1
        fn().then_inc(T.sem[sem], 1)
        note(q, reads, writes, sem)

    def dma(q, sem, out, inn, reads, writes):
        deps(q, reads, writes)
        if sem in closed:
            raise ValueError("semaphore " + sem + " was waited for already")
        cnt[sem] = cnt.get(sem, 0) + 16
        eng[q].dma_start(out, inn).then_inc(T.sem[sem], 16)
        note(q, reads, writes, sem)

    def arrived(q, sem, c):
        cnt[sem] = c
        wait(q, sem, c)

    def finish():
        for sem in sorted(cnt):
            if known["g"].get(sem, 0) < cnt[sem]:
                g.wait_ge(T.sem[sem], cnt[sem])

    return {"ap": ap, "op": op, "dma": dma, "deps": deps, "arrived": arrived, "finish": finish, "cnt": cnt}


def _relay_program(g, core, T, topo):
    for s in range(3):
        for r in range(N):
            src, dst = T.cores[r], T.cores[r ^ STEP[s]]
            way = _relays(topo, src, dst)
            if core not in way:
                continue
            i = way.index(core)
            rid, pid = topo.addr(dst, core)
            m = topo.mask(core, dst)
            n, a, b, e = _pieces(topo, src, way)[i]
            g.wait_ge(T.sem.rarr0, _count(e))
            g.remote_dma(_view(T, "land%d%s" % (s, n), a, b), _view(T, "rel" + n, a, b), T.sem["arr%d" % s], T.sem.rsent, pid, rid, m)
            g.wait_ge(T.sem.rsent, _count(m))


def rank_program(g, core, T, topo):
    rank = T.rank_of(core)
    if rank is None:
        _relay_program(g, core, T, topo)
        return
    M = _machine(g, T)
    ap, op, dma = M["ap"], M["op"], M["dma"]

    def src(inn, off):
        return ap(inn) if off is None else ap(inn).indirect(ap(off))

    def rd(*rs):
        return [r for r in rs if isinstance(r, tuple)]

    def cp(out, inn, off=None):
        op("v", lambda: g.vector.tensor_copy(ap(out), src(inn, off)), rd(inn, off), [out])

    def tt(out, a, b, o, off=None):
        op("v", lambda: g.vector.tensor_tensor(ap(out), src(a, off), ap(b), o), rd(a, b, off), [out])

    def ts(out, a, s1, s2, o0, o1=None, off=None):
        k1 = ap(s1) if isinstance(s1, tuple) else s1
        k2 = ap(s2) if isinstance(s2, tuple) else s2
        if o1 is None:
            op("v", lambda: g.vector.tensor_scalar(ap(out), src(a, off), k1, None, o0), rd(a, s1, off), [out])
        else:
            op("v", lambda: g.vector.tensor_scalar(ap(out), src(a, off), k1, k2, o0, o1), rd(a, s1, s2, off), [out])

    def act(out, inn, scale=1.0, off=None, bias=None):
        if bias is None:
            op("s", lambda: g.scalar.activation(ap(out), src(inn, off), AF.Copy, scale=scale), rd(inn, off), [out])
        else:
            op("s", lambda: g.scalar.activation(ap(out), src(inn, off), AF.Identity, bias=ap(bias), scale=scale), rd(inn, bias, off), [out])

    def fill(r, c):
        op("v", lambda: g.vector.memset(ap(r), c), [], [r])

    def tr(out, inn):
        op("v", lambda: g.vector.transpose(ap(out), ap(inn)), [inn], [out])

    def qz(n, lo, hi, tile, at=None):
        at = 4 * lo if at is None else at
        q, s, inn = V(n + "q", lo, hi), V(n + "s", lo, hi), V(tile, at, at + 4 * (hi - lo))
        op("v", lambda: g.vector.quantize_mx(ap(q), ap(s), ap(inn)), [inn], [q, s])

    def mm(ps, a, alo, b, lo, hi):
        aq, as_, bq, bs, o = V(a + "q", alo, alo + 128), V(a + "s", alo, alo + 128), V(b + "q", lo, hi), V(b + "s", lo, hi), V(ps, 0, hi - lo)
        op("t", lambda: g.tensor.matmul_mx(ap(o), ap(aq), ap(as_), ap(bq), ap(bs), True, True), [aq, as_, bq, bs], [o])

    def iota(r, pattern, base, cm, f=True):
        if f:
            op("g", lambda: g.iota(ap(r), pattern, base, cm, allow_small_or_imprecise_dtypes=True), [], [r])
        else:
            op("g", lambda: g.iota(ap(r), pattern, base, cm), [], [r])

    def sel(out, inn, pattern, o, base, cm):
        op("g", lambda: g.affine_select(ap(out), ap(inn), pattern, o, 0.0, base, cm), [inn], [out])

    def R(n, lo=0, hi=C, p0=0, p1=128):
        if n in PADDED:
            at = PAD + PADDED.index(n) * (C + PAD)
            return V("rows", at + lo, at + hi, 1, p0, p1)
        return V(n, lo, hi, 1, p0, p1)

    def W(n):
        return V(n, 0, 20)

    L16, ODD, EVEN, H1, HH, HO, T1, K1, LESS, HALF = [V("cols", k, k + 1) for k in range(10)]
    STILL = 2 * C + 2 * PAD
    TURNED = V("turned", 0, STILL + 20)

    def pick(out, win, off, o, lo, hi, scalar):
        a = (R(out, 16 * lo, 16 * hi), R(win))
        if scalar:
            act(a[0], a[1], 1.0, V(off, o + lo, o + hi))
        else:
            cp(a[0], a[1], V(off, o + lo, o + hi))

    def gather(out, win, off, o=0, cut=10, first=()):
        pick(out, win, off, o, cut, 20, True)
        for f in first:
            f()
        pick(out, win, off, o, 0, cut, False)

    def pad(k):
        fill(V("rows", k * (C + PAD), k * (C + PAD) + PAD), 0.0)

    def turn(row, cuts=(0, C)):
        for lo, hi in zip(cuts, cuts[1:]):
            more = 2 * PAD * (hi == C)
            tr(V("turned", lo, hi), R(row, lo, hi))
            tr(V("turned", C + lo, C + hi + more), R(row, lo - PAD, hi - PAD + more))

    def entries(out, cl, lo, hi):
        ts(V(out, 0, 16 * (hi - lo)), TURNED, 160.0, None, OP.add, None, V(cl, lo, hi))

    dma("y", "dq", T.gqi[:], T.gq[:], [], [W("gqi")])
    dma("s", "dm", T.gmi[:], T.gm[:], [], [W("gmi")])
    dma("y", "dx", T.x0[:], T.x[:], [], [V("x0", 0, 4 * C)])
    dma("s", "du", T.ut[:, 64:512], T.u[:, 0:448], [], [V("ut", 64, 512)])
    dma("s", "du", T.ut[:, 0:64], T.u[:, 448:512], [], [V("ut", 0, 64)])
    dma("y", "dw", T.wmq[:, 0:512].bitcast(dt.uint8), T.wc[:, 0:2048], [V("x0", 0, 4 * C)], [V("wmq", 0, 512)])
    dma("y", "dw", T.wms[:, 0:512], T.ws[:, 0:512], [], [V("wms", 0, 512)])
    IDENT = R("ident")
    pid, i0, i1, i2 = [V("ints", k, k + 1) for k in range(4)]
    iota(pid, [[1, 1]], 0, 1, False)
    iota(W("w16"), [[16, 20]], 0, 0)
    iota(IDENT, [[1, C]], -160, 0)
    iota(R("mix"), [[1, C]], -160, 0)
    iota(V("i80", 0, 80), [[0, 4], [16, 20]], 0, 0)
    iota(V("ones", 0, 516), [[0, 516]], 1, 0)
    sel(V("et", 0, 516), V("ones", 0, 516), [[1, 516]], OP.is_equal, -3, -4)
    iota(R("ash"), [[1, C]], -160, 0)
    ts(i0, pid, 15, None, OP.bitwise_and)
    ts(i1, pid, 4, 1, OP.arith_shift_right, OP.bitwise_and)
    ts(i2, pid, 1, None, OP.bitwise_and)
    cp(L16, i0)
    cp(ODD, i1)
    ts(T1, i2, -672.0, 320.0, OP.mult, OP.add)
    ts(H1, i2, 336.0, None, OP.mult)
    ts(W("wi"), W("w16"), L16, None, OP.add)
    ts(HH, T1, ODD, H1, OP.mult, OP.add)
    ts(EVEN, i1, -1.0, 1.0, OP.mult, OP.add)
    J = V("wi", 0, 4)
    J16, B1, B2, B3, Z, U, F1, F2 = [V("t32", 4 * k, 4 * k + 4) for k in range(8)]
    ts(J16, J, 59.0, 16.0, OP.min, OP.mult)
    ts(B1, J, 20.0, -320.0, OP.is_ge, OP.mult)
    ts(B2, J, 40.0, -320.0, OP.is_ge, OP.mult)
    ts(K1, HH, -1.0, float(STILL), OP.mult, OP.add)
    ts(HO, ODD, 16.0, HH, OP.mult, OP.add)
    tt(J16, J16, B1, OP.add)
    ts(B3, J, 19.0, 16.0, OP.min, OP.mult)
    ts(U, J, -15.0, K1, OP.mult, OP.add)
    tt(J16, J16, B2, OP.add)
    ts(Z, J, 20.0, None, OP.is_lt)
    ts(B2, J, 40.0, 16.0, OP.is_ge, OP.mult)
    ts(V("own", 0, 2), V("t32", 12, 14), HO, None, OP.add)
    ts(F1, U, EVEN, None, OP.mult)
    ts(V("turned", STILL, STILL + 20), W("wi"), -160.0, None, OP.add)
    tt(B1, J16, B2, OP.add)
    tt(F1, F1, Z, OP.mult)
    ts(F2, U, -16.0, ODD, OP.add, OP.mult)
    tt(B1, B1, F1, OP.add)
    cp(W("ql"), W("gqi"))
    cp(W("ml"), W("gmi"))
    tt(W("kap"), W("gmi"), W("wi"), OP.min)
    gather("ar", "ident", "ql")
    cp(W("kn"), W("kap"))
    act(R("br"), R("ar"), 1.0, W("ml"))
    act(R("kr"), IDENT, 1.0, W("kn"))
    dma("y", "dk", T.mix[1:128:16, 0:C], T.kr[1:128:16, 0:C], [R("kr")], [R("mix")])
    dma("y", "dv", T.vt[:], T.v[:], [], [V("vt", 0, 512)])
    act(R("mr"), IDENT, 1.0, W("ml"))
    ts(V("clo", 0, 4), B1, HH, None, OP.add)
    pad(0)
    pad(1)

    def halves(X):
        for b in range(4):
            act(V("xh", C * b, C * b + C), V(X, b, 4 * C, 4), 0.5)
            o = V("xi", 2 * C + b // 2, 4 * C, 2) if b % 2 else V("xi", C * b // 2, C * b // 2 + C)
            sel(o, V("xh", C * b, C * b + C), [[0, C]], OP.is_gt, 1, 0)

    def scores(xm, k):
        mm("ps%d" % (4 + k), "u2", 0, xm, PARTS[k][0], PARTS[k][1])

    def still(off, lo, hi):
        ts(V(off, lo, hi), V("i80", 0, hi - lo), L16, None, OP.add)

    qz("u2", 0, 128, "ut")
    for k, (a, b) in enumerate(PARTS):
        qz("xm", a, b, "x0")
        scores("xm", k)
    halves("x0")
    tt(R("do"), R("br"), R("ar"), OP.subtract)

    def places(kx, d, a, cl, off, first, between):
        def side(k):
            for f in between[k]:
                f()
        for k, (lo, hi) in enumerate(PARTS):
            if first:
                ts(V("sg", lo, hi), V("ps%d" % (4 + k), 0, hi - lo), 0.0, None, OP.is_gt)
            else:
                ts(V("sg", lo, hi), V("ps%d" % (4 + k), 0, hi - lo), 0.0, 0.5, OP.is_gt, OP.subtract)
        side(0)
        for h in range(2):
            tt(R("ys", 160 * h, 160 * h + 160), R("sg"), R(d, 160 * h, 160 * h + 160), OP.mult, V(kx, 10 * h, 10 * h + 10))
        for h in range(2):
            tt(R("tab", 160 * h, 160 * h + 160), R("ys", 160 * h, 160 * h + 160), R(a, 160 * h, 160 * h + 160), OP.add)
        side(1)
        turn("tab", (0, 160, C))
        side(2)
        entries(off, cl, 0, 4)
        side(3)

    def move(off, down, a, n, d, at, lo, hi, frm=None):
        f, t = (a, a + 32 * d) if down else (128 - a - n, 128 - a - n - 32 * d)
        return lambda: cp(V(off, at, at + hi - lo, 1, t, t + n), V(frm or off, lo, hi, 1, f, f + n))

    def chain(off, cl, down, last, far, cut, beside):
        beside = iter(beside + [[]] * 5)

        def side():
            for f in next(beside):
                f()
        gather("two", "tab", off, 0, cut, [move(off, down, a, 32, 1, NEXT, 20, 60) for a in (0, 32, 64)])
        pick("ra", "two", off, NEXT + 20, 0, 20, True)
        pick("rb", "ra", off, NEXT, 6, 20, True)
        side()
        turn("two")
        side()
        entries("pc", cl, 2, 4)
        side()
        for d in (2, 3):
            move(off, down, 0, 128 - 32 * d, d, far[d - 2], 8, 28, "pc")()
        pick("rb", "ra", off, NEXT, 0, 6, False)
        side()
        gather("ra", "rb", off, far[0])
        side()
        gather(last, "ra", off, far[1])

    def long_chain():
        gather("two", "tab", "offo", 0, 6, [move("offo", True, a, 32, 1, NEXT, 20, 60) for a in (0, 32, 64)])
        move("offo", True, 0, 64, 2, FAR[0], 20, FAR[0])()
        cur = "two"
        for n, o in enumerate([NEXT + 20, NEXT, FAR[0] + 20, FAR[0], FAR[1] + 20]):
            pick(("ra", "rb")[n % 2], cur, "offo", o, 0, 20, True)
            cur = ("ra", "rb")[n % 2]
        pad(3)
        pad(4)
        w = R("inv")
        op("v", lambda: g.vector.tensor_copy(ap(w).indirect(T.ql[:, 0:20]), ap(R("mix"))), [R("mix"), W("ql")], [w])
        ts(V("own", 2, 4), V("t32", 12, 14), HO, 1.0, OP.add, OP.add)
        turn("inv")
        qz("em", 0, 128, "et", 3)
        entries("n0l", "own", 0, 2)
        entries("kxb", "own", 2, 4)
        tt(R("db"), R("mr"), w, OP.subtract, W("n0l"))
        for b in range(1, 4):
            qz("em", 128 * b, 128 * b + 128, "et", 3 - b)
        qz("vw", 0, 128, "vt")
        gather("wra", cur, "offo", FAR[1])

    def send(rnd, k):
        hm, partner = "hm%d" % rnd, T.cores[rank ^ STEP[rnd]]
        way = _relays(topo, core, partner)
        qz(hm, PARTS[k][0], PARTS[k][1], "hh")
        if way:
            go = [(way[i], "rel", "rarr0", _pieces(topo, core, way)[i]) for i in ([0], [1, 2])[k]]
        else:
            m = topo.mask(core, partner)
            go = [(partner, "land%d" % rnd, "arr%d" % rnd, (n, 0, C, m)) for n in ("", "qs")[k]]
        for to, land, arr, (n, a, b, m) in go:
            M["deps"]("g", [V(hm + n, a, b)], [])
            rid, p = topo.addr(to, core)
            g.remote_dma(_view(T, land + n, a, b), _view(T, hm + n, a, b), T.sem[arr], T.sem.sent, p, rid, m)
            M["cnt"]["sent"] = M["cnt"].get("sent", 0) + _count(m)

    def fourths(out, a, b, o):
        return [[lambda h=h: tt(R(out, h, h + 80), R(a, h, h + 80), R(b, h, h + 80), o)] for h in range(0, C, 80)]

    def mean(j, k):
        a, b = PARTS[k]
        win, l = V("xh", C * j, C * j + C), V("aoff", a // 16, b // 16)
        if j % 2:
            act(V("odd", 2 * a + j // 2, 2 * b, 2), win, 1.0, l)
        else:
            tt(V("vv", 4 * a + j, 4 * b, 4), win, V("xi", C * j // 2 + a, C * j // 2 + b), OP.add, l)

    def join(k):
        a, b = PARTS[k]
        tt(V("vv", 4 * a + 1, 4 * b, 2), V("odd", 2 * a, 2 * b), V("xi", 2 * C + 2 * a, 2 * C + 2 * b), OP.add)

    def layer(k):
        a, b = PARTS[k]
        qz("vm", a, b, "vv")
        scores("vm", k)
        for j in range(4):
            ps = "ps%d" % ((0, 1, 2, 3), (6, 7, 0, 1))[k][j]
            mm(ps, "wm", 128 * j, "vm", a, b)
            act(V("hh", 4 * a + j, 4 * b, 4), V(ps, 0, b - a), 0.03125)

    for rnd in range(3):
        Y, land = "x%d" % (1 + rnd % 2), "land%d" % rnd
        partner = T.cores[rank ^ STEP[rnd]]
        if rnd == 0:
            places("kn", "do", "ar", "clo", "offo", True, [[lambda: still("offo", NEXT, NEXT + 80)], [], [lambda: still("offo", FAR[1], FAR[1] + 40)], [lambda: pad(2)]])
            long_chain()
            act(R("ah"), R("ar"), 0.5)
            act(R("bh"), R("br"), 0.5)
        else:
            a, b = fourths("mb", "nh", "mh", OP.add) if rnd == 1 else [[]] * 4, fourths("db", "db", "fb", OP.mult)
            places("kn", "do", "mo", "clo", "offo", False, [a[0], [], a[1], a[2]])
            chain("offo", "clo", True, "wra", FAR, 6, [a[3]] + b)
        turn("wra")
        if rnd == 0:
            still("offb", NEXT, NEXT + 80)
        entries("aoff", "own", 0, 2)
        if rnd == 0:
            pad(5)
            tt(B2, J16, B2, OP.subtract)
        dma("y", "ashs%d" % rnd, T.ash[16:128:16, 0:C], T.rows[0:112:16, R("wra")[1]:R("wra")[2]], [R("wra")], [R("ash")])
        for k in (96, 112):
            dma("y", "a8s%d" % rnd, T.a8[k:k + 16, 0:20], T.aoff[112:128, 0:20], [V("aoff", 0, 20, 1, 112, 128)], [V("a8", 0, 20, 1, k, k + 16)])
        for j, k in ((0, 0), (1, 0), (2, 0), (3, 0), (0, 1), (1, 1), (3, 1)):
            mean(j, k)
        join(0)
        mean(2, 1)
        layer(0)
        join(1)
        if rnd == 0:
            tt(F2, F2, Z, OP.mult)
            fill(LESS, -1.0)
        layer(1)
        more = [[]] * 4
        if rnd == 0:
            act(R("nh"), R("inv"), 0.5)
            act(R("mh"), R("mr"), 0.5, W("n0l"))
            tt(B2, B2, F2, OP.add)
            more = fourths("mo", "ah", "bh", OP.add)
        if rnd == 1:
            more = [[lambda h=h: ts(R("mq", h, h + 160), R("mo", h, h + 160), 160.0, None, OP.add)] for h in (0, 160)] + [[lambda: fill(HALF, 0.5)], []]
        places("kxb", "db", "mb" if rnd else "inv", "clb", "offb", rnd == 0,
               [[lambda: ts(V("clb", 0, 4), B2, HH, 16.0, OP.add, OP.add)] * (rnd == 0), [], [lambda: send(rnd, 0)], [lambda: send(rnd, 1)]])
        spread = [lambda q=q: cp(V("a8", 0, 20, 1, 32 * q, 32 * q + 32), V("a8", 0, 20, 1, 96, 128)) for q in range(3)]
        chain("offb", "clb", False, "rb", (FAR[0], FAR[0] + 20), 4, [more[0], spread[:2], spread[2:], more[1], more[2]])
        for f in more[3]:
            f()
        gather("wrb", "rb", "a8")
        turn("wrb")
        tt(R("ee", 0, 160), R("wrb", 0, 160), R("ash", 0, 160), OP.is_equal)
        entries("boff", "own", 0, 2)
        tt(R("ee", 160, C), R("wrb", 160, C), R("ash", 160, C), OP.is_equal)
        way = _relays(topo, partner, core) or [partner, partner]
        M["arrived"]("t", "arr%d" % rnd, sum(_count(topo.mask(k, core)) for k in way))
        for ps, j, a, b in [(0, 0) + PARTS[0], (4, 0) + PARTS[1]] + [(j, j, 0, C) for j in range(1, 4)]:
            mm("ps%d" % ps, "em", 128 * j, land, a, b)
            act(V("dsb", C * j + a, C * j + b), V("ps%d" % ps, 0, b - a))
        act(V("odd", 0, C), V("dsb", 3 * C, 4 * C), 1.0, W("boff"))
        if rnd < 2:
            act(R("fo"), R("ee"), 2.0, W("kn"), LESS)
        else:
            act(R("fo"), R("ee"), -1.0, W("kn"), HALF)
        for j in range(3):
            tt(V(Y, j, 4 * C, 4), V("dsb", C * j, C * j + C), V("vv", j, 4 * C, 4), OP.add, W("boff"))
        for a, b in PARTS:
            tt(V(Y, 4 * a + 3, 4 * b, 4), V("odd", a, b), V("vv", 4 * a + 3, 4 * b, 4), OP.add)
        for k, (a, b) in enumerate(PARTS):
            qz("xm", a, b, Y)
            if rnd < 2:
                scores("xm", k)
            else:
                mm("ps%d" % (4 + k), "vw", 0, "xm", a, b)
                act(V("yt", a, b), V("ps%d" % (4 + k), 0, b - a))
        tt(R("do"), R("do"), R("fo"), OP.mult)
        if rnd < 2:
            act(R("fb"), R("ee"), 2.0, W("kxb"), LESS)
            halves(Y)
    dma("y", "oend", T.oc[:, 0:4 * C], T.xmq[:, 0:C].bitcast(dt.uint8), [R("xmq")], [])
    dma("s", "oend", T.y[:], T.yt[:], [R("yt")], [])
    for k in range(4):
        dma("y", "oend", T.osc[4 * k:4 * k + 4, 0:C], T.xms[32 * k:32 * k + 4, 0:C], [R("xms")], [])
    tt(R("qf"), R("do"), R("mq"), OP.add)
    dma("y", "oend", T.qo[:], T.qf[0:128:16, 0:C], [R("qf")], [])
    M["finish"]()
